import numpy as np
import ml_dtypes


def mxq(x, axis, fmt="e4m3"):
    dtype, down = {"e4m3": (ml_dtypes.float8_e4m3fn, 7), "e5m2": (ml_dtypes.float8_e5m2, 14)}[fmt]
    v = np.moveaxis(np.asarray(x, np.float32).astype(ml_dtypes.bfloat16).astype(np.float64), axis, -1)
    blocks = v.reshape(v.shape[:-1] + (-1, 32))
    amax = np.abs(blocks).max(-1, keepdims=True)
    byte = np.maximum(np.where(amax > 0, np.frexp(amax)[1] - 1 + 127, 0) - down, 1)
    scale = np.exp2(byte - 127.0)
    codes = (blocks / scale).astype(np.float32).astype(dtype).astype(np.float64)
    return np.moveaxis((codes * scale).reshape(v.shape), -1, axis)


WIDE = False


def mx_kscale(k):
    if not WIDE:
        return np.ones(k)
    levels = np.array([30, -30])
    if k % 512:
        return np.exp2(np.random.permutation(np.resize(levels, k // 32))).repeat(32)
    a = np.empty((k // 512, 16))
    for p in range(k // 512):
        a[p, :8] = np.random.permutation(np.resize(levels, 8))
        for g in range(8):
            far = levels[np.abs(levels - a[p, g]) >= 10]
            a[p, g + 8] = far[np.random.randint(len(far))]
    return np.exp2(a.ravel()).repeat(32)


def f64(x):
    return np.asarray(x).astype(np.float64)


def striped(idx):
    return np.tile(idx.reshape(-1, 16).T, (8, 1)).astype(np.uint16)


def unstriped(offs):
    return offs[:16].T.reshape(-1).astype(np.int64)


def bf(x):
    return np.asarray(x, np.float32).astype(ml_dtypes.bfloat16)


E2M1 = np.array([0.0, 0.5, 1.0, 1.5, 2.0, 3.0, 4.0, 6.0, -0.0, -0.5, -1.0, -1.5, -2.0, -3.0, -4.0, -6.0])


def pack_weight(w, fmt):
    k, n = w.shape
    w = f64(bf(w)).reshape(k // 32, 32, n)
    amax = np.abs(w).max(1)
    if fmt in ("e4m3", "e5m2"):
        byte = np.frexp(amax)[1] - 1 + 127 - (7 if fmt == "e4m3" else 14)
    else:
        mant, ex = np.frexp(amax / 6.0)
        byte = np.where(mant > 0.5, ex, ex - 1) + 127
    byte = np.clip(np.where(amax > 0, byte, 1), 1, 254)
    scaled = (w * np.exp2(127.0 - byte)[:, None, :]).reshape(k, n).astype(np.float32)
    by_word = np.ascontiguousarray(scaled.reshape(k // 512, 128, 4, n).transpose(0, 1, 3, 2))
    if fmt in ("e4m3", "e5m2"):
        words = by_word.astype(ml_dtypes.float8_e4m3fn if fmt == "e4m3" else ml_dtypes.float8_e5m2).view(np.uint8)
    else:
        c = by_word.astype(ml_dtypes.float4_e2m1fn).view(np.uint8) & 0xF
        words = c[..., 0::2] | (c[..., 1::2] << 4)
    return np.ascontiguousarray(words), np.ascontiguousarray(byte.astype(np.uint8).reshape(k // 512, 16, n))


def unpack_weight(words, scales, fmt):
    g, p, n, _ = words.shape
    if fmt in ("e4m3", "e5m2"):
        vals = np.ascontiguousarray(words).view(ml_dtypes.float8_e4m3fn if fmt == "e4m3" else ml_dtypes.float8_e5m2).astype(np.float64)
    else:
        nib = np.empty((g, p, n, 4), np.uint8)
        nib[..., 0::2] = words & 0xF
        nib[..., 1::2] = words >> 4
        vals = E2M1[nib]
    vals = vals * np.repeat(np.exp2(scales.astype(np.float64) - 127.0), 8, axis=1)[..., None]
    return vals.transpose(0, 1, 3, 2).reshape(g * 512, n)


K, T, S, H, N = 1024, 2048, 1024, 1024, 512

def setup_inputs():
    n = np.random.standard_normal
    s = mx_kscale(K)[:, None]
    u = mx_kscale(H)[:, None]
    grads = n((K, T)) * np.exp(0.8 * n((1, T))) * s
    tab_words, tab_scales = pack_weight(grads, "e5m2")
    w2_words, w2_scales = pack_weight(1.5 * n((H, N)) / np.sqrt(H) / u, "e4m3")
    return {
        "tab_words": tab_words, "tab_scales": tab_scales,
        "offs": striped(np.random.permutation(T)[:S]),
        "w1": (n((K, H)) / np.sqrt(K) / s).astype(np.float32),
        "b1": (0.5 * n(H)).astype(np.float32),
        "gain": (np.exp(0.3 * n(H)) * u[:, 0]).astype(np.float32),
        "w2_words": w2_words, "w2_scales": w2_scales,
        "qg": n((N, S)).astype(np.float32),
    }

def reference(tab_words, tab_scales, offs, w1, b1, gain, w2_words, w2_scales, qg):
    v = unpack_weight(tab_words, tab_scales, "e5m2")[:, unstriped(offs)]
    a = (mxq(f64(w1), 0, "e4m3").T @ v) + f64(b1)[:, None]
    h = f64(gain)[:, None] / (1.0 + np.exp(-a))
    w2 = unpack_weight(w2_words, w2_scales, "e4m3")
    y = w2.T @ mxq(h, 0, "e4m3")
    return np.abs(f64(qg) * y)

@@ -1,0 +1,354 @@
+from contextlib import ExitStack
+
+import concourse.mybir as mybir
+
+K, T, S, H, N = 1024, 2048, 1024, 1024, 512
+FLOPS = 2 * K * H * S + 2 * H * N * S
+
+F32 = mybir.dt.float32
+BF16 = mybir.dt.bfloat16
+I32 = mybir.dt.int32
+U32 = mybir.dt.uint32
+U16 = mybir.dt.uint16
+U8 = mybir.dt.uint8
+E4 = mybir.dt.float8_e4m3fn_x4
+E5 = mybir.dt.float8_e5m2_x4
+ACT = mybir.ActivationFunctionType
+MULT = mybir.AluOpType.mult
+
+P = 128
+W = 512
+
+
+def tile_list_coordinate_influence_retrieval_kernel(
+    tc, tab_words, tab_scales, offs, w1, b1, gain, w2_words, w2_scales, qg, out
+):
+    nc = tc.nc
+    with ExitStack() as ctx:
+        keep = ctx.enter_context(tc.tile_pool(name="keep", bufs=1))
+        ring = ctx.enter_context(tc.tile_pool(name="ring", bufs=2))
+        ring3 = ctx.enter_context(tc.tile_pool(name="ring3", bufs=3))
+        ps = ctx.enter_context(tc.psum_pool(name="ps", bufs=8))
+
+        offsets = keep.tile([P, S // 16], U16, name="offsets")
+        nc.sync.dma_start(offsets[:], offs)
+
+        raw = {}
+        tabw = {}
+        late = {}
+        qs = {}
+        gs = {}
+        gw = {}
+        wg = {}
+        w1c = {}
+        w1s = {}
+        sig = {}
+        hb = {}
+        hc = {}
+        hs = {}
+        acc1 = {}
+        acc2 = {}
+        prod = {}
+
+        def load_w1(a, b):
+            raw[a, b] = ring.tile([P, 4, W], F32, name="raw", align_bytes=64)
+            nc.sync.dma_start(
+                out=raw[a, b][:],
+                in_=w1[W * a : W * (a + 1), W * b : W * (b + 1)].rearrange("(p i) r -> p i r", i=4),
+            )
+
+        def load_tab(a):
+            tabw[a] = keep.tile([P, T], I32, name="tabw", align_bytes=64)
+            nc.sync.dma_start(out=tabw[a][:], in_=tab_words[a].rearrange("p t i -> p (t i)").bitcast(I32))
+
+        bias = keep.tile([P, 2, 4], F32, name="bias")
+        nc.sync.dma_start(out=bias[:], in_=b1.rearrange("(b p t) -> p b t", p=P, t=4))
+        gtile = keep.tile([P, 2, 4], F32, name="gtile")
+        nc.sync.dma_start(out=gtile[:], in_=gain.rearrange("(b p t) -> p b t", p=P, t=4))
+        gains = gtile[:]
+
+        warm = keep.tile([P, 8], F32, name="tabw", align_bytes=64)
+        warm_out = ring.tile([P, 8], F32, name="raw", align_bytes=64)
+        warm_bias = ring.tile([P, 8], F32, name="raw", align_bytes=64)
+        tabs = keep.tile([P, T // 4], I32, name="tabs", align_bytes=64)
+        nc.vector.memset(tabs[:], 0)
+        tabw[0] = keep.tile([P, T], I32, name="tabw0", align_bytes=64)
+        nc.sync.dma_start(out=tabw[0][:], in_=tab_words[0].rearrange("p t i -> p (t i)").bitcast(I32))
+        for q in range(4):
+            nc.sync.dma_start(
+                out=tabs[32 * q : 32 * q + 8, :],
+                in_=tab_scales[:, 4 * q : 4 * q + 4, :].bitcast(I32),
+            )
+        nc.vector.memset(warm[:], 0.0)
+        nc.vector.memset(warm_bias[:], 0.0)
+        nc.scalar.activation(warm_out[:], warm[:], ACT.Sigmoid, bias=warm_bias[:, 0:1])
+        gboth = keep.tile([P, S], U8, name="gboth", align_bytes=64)
+        gmoved = keep.tile([P, S // 4], I32, name="gmoved", align_bytes=64)
+        nc.vector.memset(gmoved[:], 0)
+        for jh in range(2):
+            gs[0, jh] = gboth[:, W * jh : W * (jh + 1)]
+            gs[1, jh] = gmoved[:].bitcast(U8)[:, W * jh : W * (jh + 1)]
+
+        def gather_both(jh):
+            nc.vector.tensor_copy(gs[0, jh], tabs[:].bitcast(U8).indirect(offsets[:, 32 * jh : 32 * (jh + 1)]))
+
+        def move_scales():
+            for q in range(4):
+                nc.sync.dma_start(
+                    out=gmoved[32 * q : 32 * q + 4, :], in_=gboth[:].bitcast(I32)[32 * q + 4 : 32 * q + 8, :]
+                )
+
+        def pool_of(tag):
+            return ring if tag == "raw" else keep
+
+        gains_v = gains
+
+        def load_w2_scales():
+            w2s = keep.tile([P, 2, N // 4], I32, name="tabs", align_bytes=64)
+            late["w2s"] = w2s
+            nc.vector.memset(w2s[:], 0)
+            for q in range(4):
+                nc.sync.dma_start(
+                    out=w2s[32 * q : 32 * q + 4, :, :],
+                    in_=w2_scales[:, 4 * q : 4 * q + 4, :].rearrange("a r c -> r a c").bitcast(I32),
+                )
+
+        def load_w2(tag):
+            late["w2w"] = pool_of(tag).tile([P, 2, N], I32, name=tag, align_bytes=64)
+            nc.sync.dma_start(out=late["w2w"][:], in_=w2_words.rearrange("a p c i -> p a (c i)").bitcast(I32))
+
+        def load_q(jh, tag):
+            qs[jh] = pool_of(tag).tile([P, 4, W], F32, name=tag, align_bytes=64)
+            nc.sync.dma_start(
+                out=qs[jh][:], in_=qg[:, W * jh : W * (jh + 1)].rearrange("(nt p) j -> p nt j", p=P)
+            )
+
+        def gather_words(a, jh):
+            gw[a, jh] = keep.tile([P, W], U32, name="gw%d%d" % (a, jh), align_bytes=64)
+            nc.vector.tensor_copy(
+                gw[a, jh][:], tabw[a][:].bitcast(U32).indirect(offsets[:, 32 * jh : 32 * (jh + 1)])
+            )
+
+        def cast_w1(a, b, copy, lo=0, hi=P):
+            if (a, b) not in wg:
+                wg[a, b] = ring.tile([P, 4 * W], BF16, name="wg", align_bytes=64)
+            copy(
+                wg[a, b][:].rearrange("p (t m i) -> p m i t", t=4, i=4)[:, lo:hi],
+                raw[a, b][:].rearrange("p i (m t) -> p m i t", t=4)[:, lo:hi],
+            )
+
+        def quant_w1(a, b):
+            w1c[a, b] = keep.tile([P, W], U32, name="w1c%d%d" % (a, b), align_bytes=64)
+            w1s[a, b] = keep.tile([P, W], U8, name="w1s%d%d" % (a, b), align_bytes=64)
+            nc.vector.quantize_mx(out=w1c[a, b][:].bitcast(E4), scales=w1s[a, b][:], in_=wg[a, b][:])
+
+        def pass1(a, b, jh, t):
+            if a == 0:
+                acc1[b, jh, t] = ps.tile([P, W], F32, name="acc")
+            cols = slice(P * t, P * (t + 1))
+            nc.tensor.matmul_mx(
+                out=acc1[b, jh, t][:],
+                lhsT=w1c[a, b][:, cols].bitcast(E4),
+                lhsT_scale=w1s[a, b][:, cols],
+                rhs=gw[a, jh][:].bitcast(E5),
+                rhs_scale=gs[a, jh],
+                start=(a == 0),
+                stop=(a == 1),
+            )
+
+        def sigmoid(b, jh, t, lo, hi):
+            if (b, jh) not in sig:
+                sig[b, jh] = ring3.tile([P, 4, W], F32, name="sig")
+            nc.scalar.activation(
+                sig[b, jh][:, t, lo:hi], acc1[b, jh, t][:, lo:hi], ACT.Sigmoid, bias=bias[:, b, t : t + 1]
+            )
+
+        def open1(b, jh, ts):
+            for t in ts:
+                pass1(0, b, jh, t)
+
+        def close1(b, jh):
+            for t in range(4):
+                if (b, jh, t) not in acc1:
+                    pass1(0, b, jh, t)
+                pass1(1, b, jh, t)
+                sigmoid(b, jh, t, 0, W)
+
+        def apply_gain(b, jh, lo, hi, engine, g):
+            if (b, jh) not in hb:
+                hb[b, jh] = ring3.tile([P, 4 * W], BF16, name="hb", align_bytes=64)
+            engine.tensor_tensor(
+                hb[b, jh][:, 4 * lo : 4 * hi].rearrange("p (c i t) -> p c t i", i=4, t=4),
+                sig[b, jh][:, :, lo:hi].rearrange("p t (c i) -> p c t i", i=4),
+                g[:, b, :].unsqueeze(1).unsqueeze(3).to_broadcast([P, (hi - lo) // 4, 4, 4]),
+                MULT,
+            )
+
+        def gain_v(b, jh, lo, hi):
+            apply_gain(b, jh, lo, hi, nc.vector, gains_v)
+
+        def gain_g(b, jh, lo, hi):
+            apply_gain(b, jh, lo, hi, nc.gpsimd, gains)
+
+        def gain_s(b, jh, lo, hi):
+            if (b, jh) not in prod:
+                prod[b, jh] = keep.tile([P, 4, W], BF16, name="hp%d%d" % (b, jh), align_bytes=64)
+            for t in range(4):
+                nc.scalar.activation(
+                    prod[b, jh][:, t, lo:hi], sig[b, jh][:, t, lo:hi], ACT.Copy, scale=gains[:, b, t : t + 1]
+                )
+
+        def inter_v(b, jh, lo, hi):
+            if (b, jh) not in hb:
+                hb[b, jh] = ring3.tile([P, 4 * W], BF16, name="hb", align_bytes=64)
+            nc.vector.tensor_copy(
+                hb[b, jh][:, 4 * lo : 4 * hi].rearrange("p (c i t) -> p c t i", i=4, t=4),
+                prod[b, jh][:, :, lo:hi].rearrange("p t (c i) -> p c t i", i=4),
+            )
+
+        def quant_h(b, jh, lo, hi):
+            if (b, jh) not in hc:
+                hc[b, jh] = keep.tile([P, W], U32, name="hc%d%d" % (b, jh), align_bytes=64)
+                hs[b, jh] = keep.tile([P, W], U8, name="hs%d%d" % (b, jh), align_bytes=64)
+            nc.vector.quantize_mx(
+                out=hc[b, jh][:, lo:hi].bitcast(E4), scales=hs[b, jh][:, lo:hi], in_=hb[b, jh][:, 4 * lo : 4 * hi]
+            )
+
+        def product2(jh, lo, hi, nts):
+            bank = ps.tile([P, len(nts), hi - lo], F32, name="acc")
+            acc2[jh, lo, nts[0]] = bank
+            for u, nt in enumerate(nts):
+                for b in range(2):
+                    nc.tensor.matmul_mx(
+                        out=bank[:, u, :],
+                        lhsT=late["w2w"][:, b, P * nt : P * (nt + 1)].bitcast(E4),
+                        lhsT_scale=late["w2s"][:, b, :].bitcast(U8)[:, P * nt : P * (nt + 1)],
+                        rhs=hc[b, jh][:, lo:hi].bitcast(E4),
+                        rhs_scale=hs[b, jh][:, lo:hi],
+                        start=(b == 0),
+                        stop=(b == 1),
+                    )
+
+        def finish(jh, lo, hi, nts):
+            shape = [P, len(nts), hi - lo]
+            tag = "%d_%d_%d" % (jh, lo, nts[0])
+            product = keep.tile(shape, F32, name="prod" + tag)
+            nc.vector.tensor_tensor(
+                product[:], acc2[jh, lo, nts[0]][:], qs[jh][:, nts[0] : nts[-1] + 1, lo:hi], MULT
+            )
+            res = keep.tile(shape, F32, name="res" + tag)
+            nc.scalar.activation(res[:], product[:], ACT.Abs)
+            nc.sync.dma_start(
+                out=out[P * nts[0] : P * (nts[-1] + 1), W * jh + lo : W * jh + hi].rearrange(
+                    "(u p) j -> p u j", p=P
+                ),
+                in_=res[:],
+            )
+
+        gather_both(0)
+        load_w1(0, 0)
+        load_w1(1, 0)
+        cast_w1(0, 0, nc.scalar.copy, 0, 128)
+        cast_w1(1, 0, nc.scalar.copy, 0, 48)
+        quant_w1(0, 0)
+        gather_words(0, 0)
+        pass1(0, 0, 0, 2)
+        cast_w1(1, 0, nc.vector.tensor_copy, 48, 128)
+        pass1(0, 0, 0, 3)
+        load_w1(0, 1)
+        pass1(0, 0, 0, 1)
+        gather_words(0, 1)
+        load_tab(1)
+        gather_both(1)
+        move_scales()
+        gather_words(1, 1)
+        pass1(0, 0, 0, 0)
+        pass1(0, 0, 1, 2)
+        gather_words(1, 0)
+        quant_w1(1, 0)
+        cast_w1(0, 1, nc.vector.tensor_copy, 0, 128)
+        pass1(1, 0, 1, 2)
+        load_w1(1, 1)
+        pass1(1, 0, 0, 2)
+        pass1(1, 0, 0, 0)
+        pass1(0, 0, 1, 0)
+        sigmoid(0, 0, 0, 0, 512)
+        sigmoid(0, 1, 2, 0, 512)
+        pass1(1, 0, 0, 3)
+        pass1(1, 0, 0, 1)
+        quant_w1(0, 1)
+        sigmoid(0, 0, 3, 0, 512)
+        sigmoid(0, 0, 1, 0, 512)
+        pass1(0, 0, 1, 1)
+        load_w2("tabw")
+        sigmoid(0, 0, 2, 0, 512)
+        pass1(1, 0, 1, 1)
+        pass1(0, 0, 1, 3)
+        pass1(0, 1, 0, 2)
+        sigmoid(0, 1, 1, 0, 512)
+        cast_w1(1, 1, nc.vector.tensor_copy, 0, 128)
+        quant_w1(1, 1)
+        pass1(0, 1, 1, 0)
+        pass1(1, 0, 1, 3)
+        pass1(0, 1, 0, 1)
+        pass1(0, 1, 0, 3)
+        pass1(1, 1, 0, 3)
+        pass1(1, 0, 1, 0)
+        sigmoid(0, 1, 0, 0, 512)
+        pass1(0, 1, 1, 3)
+        pass1(1, 1, 0, 2)
+        sigmoid(1, 0, 2, 0, 512)
+        load_q(0, "raw")
+        pass1(0, 1, 1, 1)
+        load_w2_scales()
+        pass1(0, 1, 0, 0)
+        load_q(1, "raw")
+        sigmoid(0, 1, 3, 0, 512)
+        gain_v(0, 0, 0, 512)
+        sigmoid(1, 0, 3, 0, 512)
+        pass1(1, 1, 0, 1)
+        pass1(1, 1, 0, 0)
+        pass1(0, 1, 1, 2)
+        pass1(1, 1, 1, 2)
+        pass1(1, 1, 1, 3)
+        pass1(1, 1, 1, 1)
+        sigmoid(1, 0, 0, 0, 512)
+        sigmoid(1, 1, 1, 0, 256)
+        pass1(1, 1, 1, 0)
+        sigmoid(1, 1, 2, 0, 256)
+        sigmoid(1, 0, 1, 0, 512)
+        gain_s(1, 0, 0, 256)
+        sigmoid(1, 1, 3, 0, 256)
+        inter_v(1, 0, 0, 256)
+        sigmoid(1, 1, 0, 0, 256)
+        quant_h(0, 0, 0, 512)
+        gain_s(1, 1, 0, 256)
+        sigmoid(1, 1, 0, 256, 512)
+        sigmoid(1, 1, 1, 256, 512)
+        sigmoid(1, 1, 3, 256, 512)
+        gain_v(0, 1, 0, 512)
+        sigmoid(1, 1, 2, 256, 512)
+        gain_v(1, 0, 256, 512)
+        quant_h(1, 0, 0, 512)
+        product2(0, 0, 512, [1])
+        gain_s(1, 1, 256, 512)
+        inter_v(1, 1, 0, 256)
+        product2(0, 0, 512, [3])
+        quant_h(0, 1, 0, 512)
+        inter_v(1, 1, 256, 512)
+        quant_h(1, 1, 256, 512)
+        finish(0, 0, 512, [1])
+        product2(0, 0, 512, [0])
+        quant_h(1, 1, 0, 256)
+        product2(1, 256, 512, [2,3])
+        product2(0, 0, 512, [2])
+        finish(1, 256, 512, [2,3])
+        product2(1, 0, 256, [2,3])
+        finish(1, 0, 256, [2,3])
+        product2(1, 0, 256, [0,1])
+        product2(1, 256, 512, [0,1])
+        finish(0, 0, 512, [2])
+        finish(0, 0, 512, [3])
+        finish(1, 256, 512, [0,1])
+        finish(0, 0, 512, [0])
+        finish(1, 0, 256, [0,1])

@@ -1,6 +1,7 @@
 from contextlib import ExitStack
 
 import concourse.mybir as mybir
+from concourse.masks import make_identity
 
 K, T, S, H, N = 1024, 2048, 1024, 1024, 512
 FLOPS = 2 * K * H * S + 2 * H * N * S
@@ -28,7 +29,9 @@ def tile_list_coordinate_influence_retrieval_kernel(
         keep = ctx.enter_context(tc.tile_pool(name="keep", bufs=1))
         ring = ctx.enter_context(tc.tile_pool(name="ring", bufs=2))
         ring3 = ctx.enter_context(tc.tile_pool(name="ring3", bufs=3))
-        ps = ctx.enter_context(tc.psum_pool(name="ps", bufs=8))
+        ring4 = ctx.enter_context(tc.tile_pool(name="ring4", bufs=4))
+        ps = ctx.enter_context(tc.psum_pool(name="ps", bufs=7))
+        psg = ctx.enter_context(tc.psum_pool(name="psg", bufs=1))
 
         offsets = keep.tile([P, S // 16], U16, name="offsets")
         nc.sync.dma_start(offsets[:], offs)
@@ -51,7 +54,7 @@ def tile_list_coordinate_influence_retrieval_kernel(
         prod = {}
 
         def load_w1(a, b):
-            raw[a, b] = ring.tile([P, 4, W], F32, name="raw", align_bytes=64)
+            raw[a, b] = ring3.tile([P, 4, W], F32, name="raw", align_bytes=64)
             nc.sync.dma_start(
                 out=raw[a, b][:],
                 in_=w1[W * a : W * (a + 1), W * b : W * (b + 1)].rearrange("(p i) r -> p i r", i=4),
@@ -61,50 +64,52 @@ def tile_list_coordinate_influence_retrieval_kernel(
             tabw[a] = keep.tile([P, T], I32, name="tabw", align_bytes=64)
             nc.sync.dma_start(out=tabw[a][:], in_=tab_words[a].rearrange("p t i -> p (t i)").bitcast(I32))
 
-        bias = keep.tile([P, 2, 4], F32, name="bias")
-        nc.sync.dma_start(out=bias[:], in_=b1.rearrange("(b p t) -> p b t", p=P, t=4))
-        gtile = keep.tile([P, 2, 4], F32, name="gtile")
-        nc.sync.dma_start(out=gtile[:], in_=gain.rearrange("(b p t) -> p b t", p=P, t=4))
-        gains = gtile[:]
-
         warm = keep.tile([P, 8], F32, name="tabw", align_bytes=64)
-        warm_out = ring.tile([P, 8], F32, name="raw", align_bytes=64)
-        warm_bias = ring.tile([P, 8], F32, name="raw", align_bytes=64)
-        tabs = keep.tile([P, T // 4], I32, name="tabs", align_bytes=64)
+        warm_out = ring3.tile([P, 8], F32, name="raw", align_bytes=64)
+        warm_bias = ring3.tile([P, 8], F32, name="raw", align_bytes=64)
+        warm_scale = ring3.tile([P, 8], F32, name="raw", align_bytes=64)
+        tabs = keep.tile([P, 2, T // 4], I32, name="tabs", align_bytes=64)
         nc.vector.memset(tabs[:], 0)
         tabw[0] = keep.tile([P, T], I32, name="tabw0", align_bytes=64)
         nc.sync.dma_start(out=tabw[0][:], in_=tab_words[0].rearrange("p t i -> p (t i)").bitcast(I32))
+        bias = keep.tile([P, 2, 4], F32, name="bias")
+        nc.scalar.dma_start(out=bias[:], in_=b1.rearrange("(b p t) -> p b t", p=P, t=4))
+        gpad = keep.tile([P, P], F32, name="gpad")
+        gains = gpad[:, 0:8].rearrange("p (b t) -> p b t", t=4)
+        nc.scalar.dma_start(out=gains, in_=gain.rearrange("(b p t) -> p b t", p=P, t=4))
         for q in range(4):
             nc.sync.dma_start(
-                out=tabs[32 * q : 32 * q + 8, :],
-                in_=tab_scales[:, 4 * q : 4 * q + 4, :].bitcast(I32),
+                out=tabs[32 * q : 32 * q + 4, :, :],
+                in_=tab_scales[:, 4 * q : 4 * q + 4, :].rearrange("a r t -> r a t").bitcast(I32),
             )
         nc.vector.memset(warm[:], 0.0)
         nc.vector.memset(warm_bias[:], 0.0)
-        nc.scalar.activation(warm_out[:], warm[:], ACT.Sigmoid, bias=warm_bias[:, 0:1])
-        gboth = keep.tile([P, S], U8, name="gboth", align_bytes=64)
-        gmoved = keep.tile([P, S // 4], I32, name="gmoved", align_bytes=64)
-        nc.vector.memset(gmoved[:], 0)
-        for jh in range(2):
-            gs[0, jh] = gboth[:, W * jh : W * (jh + 1)]
-            gs[1, jh] = gmoved[:].bitcast(U8)[:, W * jh : W * (jh + 1)]
+        nc.vector.memset(warm_scale[:], 1.0)
+        nc.scalar.activation(warm_out[:], warm[:], ACT.Sigmoid, bias=warm_bias[:, 0:1], scale=warm_scale[:, 0:1])
+        nc.vector.memset(gpad[:, 8:], 0.0)
 
-        def gather_both(jh):
-            nc.vector.tensor_copy(gs[0, jh], tabs[:].bitcast(U8).indirect(offsets[:, 32 * jh : 32 * (jh + 1)]))
-
-        def move_scales():
-            for q in range(4):
-                nc.sync.dma_start(
-                    out=gmoved[32 * q : 32 * q + 4, :], in_=gboth[:].bitcast(I32)[32 * q + 4 : 32 * q + 8, :]
-                )
+        def gather_scales(a, jh):
+            plane = keep.tile([P, W], U8, name="gs%d%d" % (a, jh), align_bytes=64)
+            gs[a, jh] = plane[:]
+            nc.vector.tensor_copy(
+                gs[a, jh], tabs[:, a, :].bitcast(U8).indirect(offsets[:, 32 * jh : 32 * (jh + 1)])
+            )
 
         def pool_of(tag):
-            return ring if tag == "raw" else keep
+            return ring3 if tag == "raw" else keep
 
-        gains_v = gains
+        ident = keep.tile([P, P], F32, name="ident")
+        make_identity(nc, ident[:])
+        g_t = ps.tile([P, P], F32, name="acc")
+        nc.tensor.transpose(g_t[:], gpad[:], ident[:])
+        g_rows = keep.tile([P, P], F32, name="g_rows")
+        nc.scalar.copy(g_rows[:], g_t[:])
+        g_ps = psg.tile([P, P], F32, name="g_ps")
+        nc.tensor.transpose(g_ps[:], g_rows[:], ident[:])
+        gains_v = g_ps[:, 0:8].rearrange("p (b t) -> p b t", t=4)
 
         def load_w2_scales():
-            w2s = keep.tile([P, 2, N // 4], I32, name="tabs", align_bytes=64)
+            w2s = ring3.tile([P, 2, N // 4], I32, name="wg", align_bytes=64)
             late["w2s"] = w2s
             nc.vector.memset(w2s[:], 0)
             for q in range(4):
@@ -118,9 +123,9 @@ def tile_list_coordinate_influence_retrieval_kernel(
             nc.sync.dma_start(out=late["w2w"][:], in_=w2_words.rearrange("a p c i -> p a (c i)").bitcast(I32))
 
         def load_q(jh, tag):
-            qs[jh] = pool_of(tag).tile([P, 4, W], F32, name=tag, align_bytes=64)
+            qs[jh] = pool_of(tag).tile([P, 2, S], F32, name=tag, align_bytes=64)
             nc.sync.dma_start(
-                out=qs[jh][:], in_=qg[:, W * jh : W * (jh + 1)].rearrange("(nt p) j -> p nt j", p=P)
+                out=qs[jh][:], in_=qg[2 * P * jh : 2 * P * (jh + 1), :].rearrange("(nt p) j -> p nt j", p=P)
             )
 
         def gather_words(a, jh):
@@ -131,7 +136,7 @@ def tile_list_coordinate_influence_retrieval_kernel(
 
         def cast_w1(a, b, copy, lo=0, hi=P):
             if (a, b) not in wg:
-                wg[a, b] = ring.tile([P, 4 * W], BF16, name="wg", align_bytes=64)
+                wg[a, b] = ring3.tile([P, 4 * W], BF16, name="wg", align_bytes=64)
             copy(
                 wg[a, b][:].rearrange("p (t m i) -> p m i t", t=4, i=4)[:, lo:hi],
                 raw[a, b][:].rearrange("p i (m t) -> p m i t", t=4)[:, lo:hi],
@@ -158,7 +163,7 @@ def tile_list_coordinate_influence_retrieval_kernel(
 
         def sigmoid(b, jh, t, lo, hi):
             if (b, jh) not in sig:
-                sig[b, jh] = ring3.tile([P, 4, W], F32, name="sig")
+                sig[b, jh] = ring4.tile([P, 4, W], F32, name="sig")
             nc.scalar.activation(
                 sig[b, jh][:, t, lo:hi], acc1[b, jh, t][:, lo:hi], ACT.Sigmoid, bias=bias[:, b, t : t + 1]
             )
@@ -176,7 +181,7 @@ def tile_list_coordinate_influence_retrieval_kernel(
 
         def apply_gain(b, jh, lo, hi, engine, g):
             if (b, jh) not in hb:
-                hb[b, jh] = ring3.tile([P, 4 * W], BF16, name="hb", align_bytes=64)
+                hb[b, jh] = ring4.tile([P, 4 * W], BF16, name="hb", align_bytes=64)
             engine.tensor_tensor(
                 hb[b, jh][:, 4 * lo : 4 * hi].rearrange("p (c i t) -> p c t i", i=4, t=4),
                 sig[b, jh][:, :, lo:hi].rearrange("p t (c i) -> p c t i", i=4),
@@ -188,7 +193,14 @@ def tile_list_coordinate_influence_retrieval_kernel(
             apply_gain(b, jh, lo, hi, nc.vector, gains_v)
 
         def gain_g(b, jh, lo, hi):
-            apply_gain(b, jh, lo, hi, nc.gpsimd, gains)
+            if (b, jh) not in hb:
+                hb[b, jh] = ring4.tile([P, 4 * W], BF16, name="hb", align_bytes=64)
+            nc.gpsimd.tensor_tensor(
+                hb[b, jh][:, 4 * lo : 4 * hi].rearrange("p (n t) -> p n t", t=4),
+                sig[b, jh][:, :, lo:hi].rearrange("p t n -> p n t"),
+                gains[:, b, :].unsqueeze(1).to_broadcast([P, hi - lo, 4]),
+                MULT,
+            )
 
         def gain_s(b, jh, lo, hi):
             if (b, jh) not in prod:
@@ -200,7 +212,7 @@ def tile_list_coordinate_influence_retrieval_kernel(
 
         def inter_v(b, jh, lo, hi):
             if (b, jh) not in hb:
-                hb[b, jh] = ring3.tile([P, 4 * W], BF16, name="hb", align_bytes=64)
+                hb[b, jh] = ring4.tile([P, 4 * W], BF16, name="hb", align_bytes=64)
             nc.vector.tensor_copy(
                 hb[b, jh][:, 4 * lo : 4 * hi].rearrange("p (c i t) -> p c t i", i=4, t=4),
                 prod[b, jh][:, :, lo:hi].rearrange("p t (c i) -> p c t i", i=4),
@@ -234,7 +246,7 @@ def tile_list_coordinate_influence_retrieval_kernel(
             tag = "%d_%d_%d" % (jh, lo, nts[0])
             product = keep.tile(shape, F32, name="prod" + tag)
             nc.vector.tensor_tensor(
-                product[:], acc2[jh, lo, nts[0]][:], qs[jh][:, nts[0] : nts[-1] + 1, lo:hi], MULT
+                product[:], acc2[jh, lo, nts[0]][:], qs[nts[0] // 2][:, nts[0] % 2 : nts[-1] % 2 + 1, W * jh + lo : W * jh + hi], MULT
             )
             res = keep.tile(shape, F32, name="res" + tag)
             nc.scalar.activation(res[:], product[:], ACT.Abs)
@@ -245,110 +257,110 @@ def tile_list_coordinate_influence_retrieval_kernel(
                 in_=res[:],
             )
 
-        gather_both(0)
         load_w1(0, 0)
         load_w1(1, 0)
-        cast_w1(0, 0, nc.scalar.copy, 0, 128)
-        cast_w1(1, 0, nc.scalar.copy, 0, 48)
-        quant_w1(0, 0)
-        gather_words(0, 0)
-        pass1(0, 0, 0, 2)
-        cast_w1(1, 0, nc.vector.tensor_copy, 48, 128)
-        pass1(0, 0, 0, 3)
-        load_w1(0, 1)
-        pass1(0, 0, 0, 1)
-        gather_words(0, 1)
         load_tab(1)
-        gather_both(1)
-        move_scales()
-        gather_words(1, 1)
+        load_w1(0, 1)
+        gather_words(0, 0)
+        gather_words(0, 1)
+        gather_scales(0, 0)
+        gather_scales(0, 1)
+        cast_w1(0, 0, nc.scalar.copy, 0, 128)
+        load_w1(1, 1)
+        gather_scales(1, 0)
+        gather_scales(1, 1)
+        quant_w1(0, 0)
         pass1(0, 0, 0, 0)
+        pass1(0, 0, 0, 1)
+        pass1(0, 0, 0, 2)
+        pass1(0, 0, 0, 3)
+        pass1(0, 0, 1, 0)
+        pass1(0, 0, 1, 1)
         pass1(0, 0, 1, 2)
+        cast_w1(1, 0, nc.scalar.copy, 0, 128)
+        load_q(0, "raw")
         gather_words(1, 0)
         quant_w1(1, 0)
-        cast_w1(0, 1, nc.vector.tensor_copy, 0, 128)
-        pass1(1, 0, 1, 2)
-        load_w1(1, 1)
-        pass1(1, 0, 0, 2)
         pass1(1, 0, 0, 0)
-        pass1(0, 0, 1, 0)
-        sigmoid(0, 0, 0, 0, 512)
-        sigmoid(0, 1, 2, 0, 512)
-        pass1(1, 0, 0, 3)
         pass1(1, 0, 0, 1)
-        quant_w1(0, 1)
-        sigmoid(0, 0, 3, 0, 512)
-        sigmoid(0, 0, 1, 0, 512)
-        pass1(0, 0, 1, 1)
+        pass1(1, 0, 0, 2)
+        pass1(1, 0, 0, 3)
+        gather_words(1, 1)
+        cast_w1(0, 1, nc.scalar.copy, 0, 80)
+        cast_w1(0, 1, nc.vector.tensor_copy, 80, 128)
         load_w2("tabw")
+        load_q(1, "raw")
+        sigmoid(0, 0, 0, 0, 512)
+        sigmoid(0, 0, 1, 0, 512)
         sigmoid(0, 0, 2, 0, 512)
-        pass1(1, 0, 1, 1)
-        pass1(0, 0, 1, 3)
-        pass1(0, 1, 0, 2)
-        sigmoid(0, 1, 1, 0, 512)
+        sigmoid(0, 0, 3, 0, 512)
+        quant_w1(0, 1)
         cast_w1(1, 1, nc.vector.tensor_copy, 0, 128)
+        load_w2_scales()
         quant_w1(1, 1)
-        pass1(0, 1, 1, 0)
-        pass1(1, 0, 1, 3)
-        pass1(0, 1, 0, 1)
-        pass1(0, 1, 0, 3)
-        pass1(1, 1, 0, 3)
         pass1(1, 0, 1, 0)
         sigmoid(0, 1, 0, 0, 512)
-        pass1(0, 1, 1, 3)
+        pass1(1, 0, 1, 1)
+        sigmoid(0, 1, 1, 0, 512)
+        pass1(1, 0, 1, 2)
+        sigmoid(0, 1, 2, 0, 512)
+        pass1(0, 0, 1, 3)
+        pass1(1, 0, 1, 3)
+        sigmoid(0, 1, 3, 0, 512)
+        gain_g(0, 0, 256, 384)
+        gain_g(0, 0, 384, 512)
+        gain_g(0, 1, 384, 512)
+        pass1(0, 1, 0, 0)
+        pass1(1, 1, 0, 0)
+        sigmoid(1, 0, 0, 0, 512)
+        pass1(0, 1, 0, 1)
+        pass1(1, 1, 0, 1)
+        sigmoid(1, 0, 1, 0, 512)
+        pass1(0, 1, 0, 2)
         pass1(1, 1, 0, 2)
         sigmoid(1, 0, 2, 0, 512)
-        load_q(0, "raw")
-        pass1(0, 1, 1, 1)
-        load_w2_scales()
-        pass1(0, 1, 0, 0)
-        load_q(1, "raw")
-        sigmoid(0, 1, 3, 0, 512)
-        gain_v(0, 0, 0, 512)
+        pass1(0, 1, 0, 3)
+        pass1(1, 1, 0, 3)
         sigmoid(1, 0, 3, 0, 512)
-        pass1(1, 1, 0, 1)
-        pass1(1, 1, 0, 0)
+        gain_g(1, 0, 256, 384)
+        gain_s(1, 0, 384, 512)
+        pass1(0, 1, 1, 0)
+        pass1(1, 1, 1, 0)
+        sigmoid(1, 1, 0, 0, 512)
+        pass1(0, 1, 1, 1)
+        pass1(1, 1, 1, 1)
+        sigmoid(1, 1, 1, 0, 512)
         pass1(0, 1, 1, 2)
         pass1(1, 1, 1, 2)
+        sigmoid(1, 1, 2, 0, 512)
+        pass1(0, 1, 1, 3)
         pass1(1, 1, 1, 3)
-        pass1(1, 1, 1, 1)
-        sigmoid(1, 0, 0, 0, 512)
-        sigmoid(1, 1, 1, 0, 256)
-        pass1(1, 1, 1, 0)
-        sigmoid(1, 1, 2, 0, 256)
-        sigmoid(1, 0, 1, 0, 512)
-        gain_s(1, 0, 0, 256)
-        sigmoid(1, 1, 3, 0, 256)
-        inter_v(1, 0, 0, 256)
-        sigmoid(1, 1, 0, 0, 256)
+        sigmoid(1, 1, 3, 0, 512)
+        gain_g(1, 1, 256, 384)
+        gain_s(1, 1, 384, 512)
+        gain_v(0, 0, 0, 256)
+        gain_v(0, 1, 0, 384)
         quant_h(0, 0, 0, 512)
-        gain_s(1, 1, 0, 256)
-        sigmoid(1, 1, 0, 256, 512)
-        sigmoid(1, 1, 1, 256, 512)
-        sigmoid(1, 1, 3, 256, 512)
-        gain_v(0, 1, 0, 512)
-        sigmoid(1, 1, 2, 256, 512)
-        gain_v(1, 0, 256, 512)
+        gain_v(1, 0, 0, 256)
+        inter_v(1, 0, 384, 512)
         quant_h(1, 0, 0, 512)
-        product2(0, 0, 512, [1])
-        gain_s(1, 1, 256, 512)
-        inter_v(1, 1, 0, 256)
-        product2(0, 0, 512, [3])
         quant_h(0, 1, 0, 512)
-        inter_v(1, 1, 256, 512)
-        quant_h(1, 1, 256, 512)
-        finish(0, 0, 512, [1])
         product2(0, 0, 512, [0])
-        quant_h(1, 1, 0, 256)
-        product2(1, 256, 512, [2,3])
+        product2(0, 0, 512, [1])
         product2(0, 0, 512, [2])
-        finish(1, 256, 512, [2,3])
-        product2(1, 0, 256, [2,3])
-        finish(1, 0, 256, [2,3])
-        product2(1, 0, 256, [0,1])
-        product2(1, 256, 512, [0,1])
+        product2(0, 0, 512, [3])
+        gain_v(1, 1, 0, 256)
+        inter_v(1, 1, 384, 512)
+        finish(0, 0, 512, [0])
+        finish(0, 0, 512, [1])
+        quant_h(1, 1, 0, 512)
         finish(0, 0, 512, [2])
         finish(0, 0, 512, [3])
-        finish(1, 256, 512, [0,1])
-        finish(0, 0, 512, [0])
-        finish(1, 0, 256, [0,1])
+        product2(1, 0, 512, [0])
+        finish(1, 0, 512, [0])
+        product2(1, 0, 512, [1])
+        finish(1, 0, 512, [1])
+        product2(1, 0, 512, [2])
+        finish(1, 0, 512, [2])
+        product2(1, 0, 512, [3])
+        finish(1, 0, 512, [3])

@@ -54,7 +54,8 @@ def tile_list_coordinate_influence_retrieval_kernel(
         prod = {}
 
         def load_w1(a, b):
-            raw[a, b] = ring3.tile([P, 4, W], F32, name="raw", align_bytes=64)
+            tag = "tabs" if (a, b) == (0, 1) else "raw"
+            raw[a, b] = (ring if tag == "raw" else keep).tile([P, 4, W], F32, name=tag, align_bytes=64)
             nc.sync.dma_start(
                 out=raw[a, b][:],
                 in_=w1[W * a : W * (a + 1), W * b : W * (b + 1)].rearrange("(p i) r -> p i r", i=4),
@@ -65,10 +66,9 @@ def tile_list_coordinate_influence_retrieval_kernel(
             nc.sync.dma_start(out=tabw[a][:], in_=tab_words[a].rearrange("p t i -> p (t i)").bitcast(I32))
 
         warm = keep.tile([P, 8], F32, name="tabw", align_bytes=64)
-        warm_out = ring3.tile([P, 8], F32, name="raw", align_bytes=64)
-        warm_bias = ring3.tile([P, 8], F32, name="raw", align_bytes=64)
-        warm_scale = ring3.tile([P, 8], F32, name="raw", align_bytes=64)
-        tabs = keep.tile([P, 2, T // 4], I32, name="tabs", align_bytes=64)
+        warm_out = ring.tile([P, 8], F32, name="raw", align_bytes=64)
+        warm_bias = ring.tile([P, 8], F32, name="raw", align_bytes=64)
+        tabs = keep.tile([P, T // 4], I32, name="tabs", align_bytes=64)
         nc.vector.memset(tabs[:], 0)
         tabw[0] = keep.tile([P, T], I32, name="tabw0", align_bytes=64)
         nc.sync.dma_start(out=tabw[0][:], in_=tab_words[0].rearrange("p t i -> p (t i)").bitcast(I32))
@@ -77,26 +77,33 @@ def tile_list_coordinate_influence_retrieval_kernel(
         gpad = keep.tile([P, P], F32, name="gpad")
         gains = gpad[:, 0:8].rearrange("p (b t) -> p b t", t=4)
         nc.scalar.dma_start(out=gains, in_=gain.rearrange("(b p t) -> p b t", p=P, t=4))
-        for q in range(4):
-            nc.sync.dma_start(
-                out=tabs[32 * q : 32 * q + 4, :, :],
-                in_=tab_scales[:, 4 * q : 4 * q + 4, :].rearrange("a r t -> r a t").bitcast(I32),
-            )
+        scale_rows = tab_scales.rearrange("a q t -> (a q) t").bitcast(I32)
+        nc.sync.dma_start(out=tabs[0:32, :], in_=scale_rows)
+        for q in range(1, 4):
+            nc.sync.dma_start(out=tabs[32 * q : 32 * q + 4, :], in_=scale_rows[4 * q : 4 * q + 4, :])
         nc.vector.memset(warm[:], 0.0)
         nc.vector.memset(warm_bias[:], 0.0)
-        nc.vector.memset(warm_scale[:], 1.0)
-        nc.scalar.activation(warm_out[:], warm[:], ACT.Sigmoid, bias=warm_bias[:, 0:1], scale=warm_scale[:, 0:1])
+        nc.scalar.activation(warm_out[:], warm[:], ACT.Sigmoid, bias=warm_bias[:, 0:1])
         nc.vector.memset(gpad[:, 8:], 0.0)
 
-        def gather_scales(a, jh):
-            plane = keep.tile([P, W], U8, name="gs%d%d" % (a, jh), align_bytes=64)
-            gs[a, jh] = plane[:]
-            nc.vector.tensor_copy(
-                gs[a, jh], tabs[:, a, :].bitcast(U8).indirect(offsets[:, 32 * jh : 32 * (jh + 1)])
-            )
+        gboth = keep.tile([P, S], U8, name="gboth", align_bytes=64)
+        gmoved = keep.tile([P, S // 4], I32, name="gmoved", align_bytes=64)
+        nc.vector.memset(gmoved[:], 0)
+        for jh in range(2):
+            gs[0, jh] = gboth[:, W * jh : W * (jh + 1)]
+            gs[1, jh] = gmoved[:].bitcast(U8)[:, W * jh : W * (jh + 1)]
+
+        def gather_both(jh):
+            nc.vector.tensor_copy(gs[0, jh], tabs[:].bitcast(U8).indirect(offsets[:, 32 * jh : 32 * (jh + 1)]))
+
+        def move_scales():
+            for q in range(4):
+                nc.sync.dma_start(
+                    out=gmoved[32 * q : 32 * q + 4, :], in_=gboth[:].bitcast(I32)[16 + 4 * q : 20 + 4 * q, :]
+                )
 
         def pool_of(tag):
-            return ring3 if tag == "raw" else keep
+            return ring if tag == "raw" else keep
 
         ident = keep.tile([P, P], F32, name="ident")
         make_identity(nc, ident[:])
@@ -241,6 +248,17 @@ def tile_list_coordinate_influence_retrieval_kernel(
                         stop=(b == 1),
                     )
 
+        def evac(jh, nt):
+            y = keep.tile([P, W], F32, name="y%d%d" % (jh, nt))
+            nc.scalar.copy(y[:], acc2[jh, 0, nt][:, 0, :])
+            prod["g", nt] = keep.tile([P, W], F32, name="gprod%d%d" % (jh, nt))
+            nc.gpsimd.tensor_tensor(prod["g", nt][:], y[:], qs[nt // 2][:, nt % 2, W * jh : W * (jh + 1)], MULT)
+
+        def absout(jh, nt):
+            res = keep.tile([P, W], F32, name="gres%d%d" % (jh, nt))
+            nc.scalar.activation(res[:], prod["g", nt][:], ACT.Abs)
+            nc.sync.dma_start(out=out[P * nt : P * (nt + 1), W * jh : W * (jh + 1)], in_=res[:])
+
         def finish(jh, lo, hi, nts):
             shape = [P, len(nts), hi - lo]
             tag = "%d_%d_%d" % (jh, lo, nts[0])
@@ -260,15 +278,14 @@ def tile_list_coordinate_influence_retrieval_kernel(
         load_w1(0, 0)
         load_w1(1, 0)
         load_tab(1)
+        gather_both(0)
+        gather_both(1)
+        move_scales()
         load_w1(0, 1)
-        gather_words(0, 0)
         gather_words(0, 1)
-        gather_scales(0, 0)
-        gather_scales(0, 1)
+        gather_words(0, 0)
         cast_w1(0, 0, nc.scalar.copy, 0, 128)
         load_w1(1, 1)
-        gather_scales(1, 0)
-        gather_scales(1, 1)
         quant_w1(0, 0)
         pass1(0, 0, 0, 0)
         pass1(0, 0, 0, 1)
@@ -277,25 +294,27 @@ def tile_list_coordinate_influence_retrieval_kernel(
         pass1(0, 0, 1, 0)
         pass1(0, 0, 1, 1)
         pass1(0, 0, 1, 2)
-        cast_w1(1, 0, nc.scalar.copy, 0, 128)
+        cast_w1(1, 0, nc.scalar.copy, 0, 48)
+        cast_w1(1, 0, nc.vector.tensor_copy, 48, 128)
         load_q(0, "raw")
-        gather_words(1, 0)
         quant_w1(1, 0)
+        gather_words(1, 0)
         pass1(1, 0, 0, 0)
         pass1(1, 0, 0, 1)
         pass1(1, 0, 0, 2)
         pass1(1, 0, 0, 3)
         gather_words(1, 1)
-        cast_w1(0, 1, nc.scalar.copy, 0, 80)
-        cast_w1(0, 1, nc.vector.tensor_copy, 80, 128)
+        cast_w1(0, 1, nc.scalar.copy, 0, 32)
+        cast_w1(0, 1, nc.vector.tensor_copy, 32, 128)
         load_w2("tabw")
-        load_q(1, "raw")
         sigmoid(0, 0, 0, 0, 512)
         sigmoid(0, 0, 1, 0, 512)
         sigmoid(0, 0, 2, 0, 512)
         sigmoid(0, 0, 3, 0, 512)
         quant_w1(0, 1)
-        cast_w1(1, 1, nc.vector.tensor_copy, 0, 128)
+        cast_w1(1, 1, nc.scalar.copy, 0, 32)
+        cast_w1(1, 1, nc.vector.tensor_copy, 32, 128)
+        load_q(1, "raw")
         load_w2_scales()
         quant_w1(1, 1)
         pass1(1, 0, 1, 0)
@@ -307,8 +326,8 @@ def tile_list_coordinate_influence_retrieval_kernel(
         pass1(0, 0, 1, 3)
         pass1(1, 0, 1, 3)
         sigmoid(0, 1, 3, 0, 512)
-        gain_g(0, 0, 256, 384)
         gain_g(0, 0, 384, 512)
+        gain_g(0, 1, 256, 384)
         gain_g(0, 1, 384, 512)
         pass1(0, 1, 0, 0)
         pass1(1, 1, 0, 0)
@@ -336,10 +355,9 @@ def tile_list_coordinate_influence_retrieval_kernel(
         pass1(0, 1, 1, 3)
         pass1(1, 1, 1, 3)
         sigmoid(1, 1, 3, 0, 512)
-        gain_g(1, 1, 256, 384)
-        gain_s(1, 1, 384, 512)
-        gain_v(0, 0, 0, 256)
-        gain_v(0, 1, 0, 384)
+        gain_g(1, 1, 384, 512)
+        gain_v(0, 0, 0, 384)
+        gain_v(0, 1, 0, 256)
         quant_h(0, 0, 0, 512)
         gain_v(1, 0, 0, 256)
         inter_v(1, 0, 384, 512)
@@ -349,9 +367,9 @@ def tile_list_coordinate_influence_retrieval_kernel(
         product2(0, 0, 512, [1])
         product2(0, 0, 512, [2])
         product2(0, 0, 512, [3])
-        gain_v(1, 1, 0, 256)
-        inter_v(1, 1, 384, 512)
-        finish(0, 0, 512, [0])
+        evac(0, 0)
+        gain_v(1, 1, 0, 384)
+        absout(0, 0)
         finish(0, 0, 512, [1])
         quant_h(1, 1, 0, 512)
         finish(0, 0, 512, [2])

@@ -12,13 +12,27 @@ I32 = mybir.dt.int32
 U32 = mybir.dt.uint32
 U16 = mybir.dt.uint16
 U8 = mybir.dt.uint8
-E4 = mybir.dt.float8_e4m3fn_x4
-E5 = mybir.dt.float8_e5m2_x4
+E4M3 = mybir.dt.float8_e4m3fn_x4
+E5M2 = mybir.dt.float8_e5m2_x4
 ACT = mybir.ActivationFunctionType
 MULT = mybir.AluOpType.mult
 
 P = 128
+PACK = 4
 W = 512
+LIST_COLS = W // 16
+QUADRANT = 32
+RUN = 4
+PASS1_ROW = 16
+LINE = 4
+SLOTS = range(PACK)
+ROW_TILES = range(N // P)
+GAINS = 2 * PACK
+SUM_BANKS = 7
+
+ROUND_ON_SCALAR = {(0, 0): 128, (1, 0): 48, (0, 1): 32, (1, 1): 32}
+GAIN_CUTS = {(0, 0): (384, 512), (0, 1): (256, 512), (1, 0): (256, 384), (1, 1): (384, 512)}
+GPSIMD_COLS = 128
 
 
 def tile_list_coordinate_influence_retrieval_kernel(
@@ -27,358 +41,279 @@ def tile_list_coordinate_influence_retrieval_kernel(
     nc = tc.nc
     with ExitStack() as ctx:
         keep = ctx.enter_context(tc.tile_pool(name="keep", bufs=1))
-        ring = ctx.enter_context(tc.tile_pool(name="ring", bufs=2))
-        ring3 = ctx.enter_context(tc.tile_pool(name="ring3", bufs=3))
-        ring4 = ctx.enter_context(tc.tile_pool(name="ring4", bufs=4))
-        ps = ctx.enter_context(tc.psum_pool(name="ps", bufs=7))
-        psg = ctx.enter_context(tc.psum_pool(name="psg", bufs=1))
+        stage = ctx.enter_context(tc.tile_pool(name="stage", bufs=2))
+        rounded = ctx.enter_context(tc.tile_pool(name="rounded", bufs=3))
+        hidden = ctx.enter_context(tc.tile_pool(name="hidden", bufs=4))
+        sums = ctx.enter_context(tc.psum_pool(name="sums", bufs=SUM_BANKS))
+        gain_bank = ctx.enter_context(tc.psum_pool(name="gain_bank", bufs=1))
+
+        def buffer(tag, shape, dtype):
+            return (stage if tag == "stage" else keep).tile(shape, dtype, name=tag, align_bytes=64)
 
         offsets = keep.tile([P, S // 16], U16, name="offsets")
         nc.sync.dma_start(offsets[:], offs)
 
-        raw = {}
-        tabw = {}
-        late = {}
-        qs = {}
-        gs = {}
-        gw = {}
-        wg = {}
-        w1c = {}
-        w1s = {}
-        sig = {}
-        hb = {}
-        hc = {}
-        hs = {}
-        acc1 = {}
-        acc2 = {}
-        prod = {}
+        def half_of_list(jh):
+            return offsets[:, LIST_COLS * jh : LIST_COLS * (jh + 1)]
 
-        def load_w1(a, b):
-            tag = "tabs" if (a, b) == (0, 1) else "raw"
-            raw[a, b] = (ring if tag == "raw" else keep).tile([P, 4, W], F32, name=tag, align_bytes=64)
+        table = {}
+
+        def load_table(a, tag):
+            table[a] = buffer(tag, [P, T], I32)
+            nc.sync.dma_start(out=table[a][:], in_=tab_words[a].rearrange("p t i -> p (t i)").bitcast(I32))
+
+        filler_in = buffer("words1", [P, P - GAINS], F32)
+        filler_bias = buffer("stage", [P, 1], F32)
+        filler_scale = buffer("stage", [P, 1], F32)
+
+        scale_window = buffer("scale_window", [P, T // 4], I32)
+        nc.vector.memset(scale_window[:], 0)
+        load_table(0, "words0")
+        bias = keep.tile([P, 2, PACK], F32, name="bias")
+        nc.scalar.dma_start(out=bias[:], in_=b1.rearrange("(b p t) -> p b t", p=P, t=PACK))
+        gain_square = keep.tile([P, P], F32, name="gain_square")
+        gains = gain_square[:, 0:GAINS].rearrange("p (b t) -> p b t", t=PACK)
+        nc.scalar.dma_start(out=gains, in_=gain.rearrange("(b p t) -> p b t", p=P, t=PACK))
+        scale_rows = tab_scales.rearrange("a q t -> (a q) t").bitcast(I32)
+        nc.sync.dma_start(out=scale_window[0:QUADRANT, :], in_=scale_rows)
+        for q in range(1, 4):
             nc.sync.dma_start(
-                out=raw[a, b][:],
-                in_=w1[W * a : W * (a + 1), W * b : W * (b + 1)].rearrange("(p i) r -> p i r", i=4),
+                out=scale_window[QUADRANT * q : QUADRANT * q + RUN, :], in_=scale_rows[RUN * q : RUN * (q + 1), :]
             )
 
-        def load_tab(a):
-            tabw[a] = keep.tile([P, T], I32, name="tabw", align_bytes=64)
-            nc.sync.dma_start(out=tabw[a][:], in_=tab_words[a].rearrange("p t i -> p (t i)").bitcast(I32))
+        nc.vector.memset(filler_in[:], 0.0)
+        nc.vector.memset(filler_bias[:], 0.0)
+        nc.vector.memset(filler_scale[:], 1.0)
+        nc.scalar.activation(
+            gain_square[:, GAINS:], filler_in[:], ACT.Sigmoid, bias=filler_bias[:], scale=filler_scale[:]
+        )
 
-        warm = keep.tile([P, 8], F32, name="tabw", align_bytes=64)
-        warm_out = ring.tile([P, 8], F32, name="raw", align_bytes=64)
-        warm_bias = ring.tile([P, 8], F32, name="raw", align_bytes=64)
-        tabs = keep.tile([P, T // 4], I32, name="tabs", align_bytes=64)
-        nc.vector.memset(tabs[:], 0)
-        tabw[0] = keep.tile([P, T], I32, name="tabw0", align_bytes=64)
-        nc.sync.dma_start(out=tabw[0][:], in_=tab_words[0].rearrange("p t i -> p (t i)").bitcast(I32))
-        bias = keep.tile([P, 2, 4], F32, name="bias")
-        nc.scalar.dma_start(out=bias[:], in_=b1.rearrange("(b p t) -> p b t", p=P, t=4))
-        gpad = keep.tile([P, P], F32, name="gpad")
-        gains = gpad[:, 0:8].rearrange("p (b t) -> p b t", t=4)
-        nc.scalar.dma_start(out=gains, in_=gain.rearrange("(b p t) -> p b t", p=P, t=4))
-        scale_rows = tab_scales.rearrange("a q t -> (a q) t").bitcast(I32)
-        nc.sync.dma_start(out=tabs[0:32, :], in_=scale_rows)
-        for q in range(1, 4):
-            nc.sync.dma_start(out=tabs[32 * q : 32 * q + 4, :], in_=scale_rows[4 * q : 4 * q + 4, :])
-        nc.vector.memset(warm[:], 0.0)
-        nc.vector.memset(warm_bias[:], 0.0)
-        nc.scalar.activation(warm_out[:], warm[:], ACT.Sigmoid, bias=warm_bias[:, 0:1])
-        nc.vector.memset(gpad[:, 8:], 0.0)
+        picked_scales = keep.tile([P, S], U8, name="picked_scales", align_bytes=64)
+        moved_scales = keep.tile([P, S // 4], I32, name="moved_scales", align_bytes=64)
+        nc.vector.memset(moved_scales[:], 0)
+        v_plane = {0: picked_scales[:], 1: moved_scales[:].bitcast(U8)}
 
-        gboth = keep.tile([P, S], U8, name="gboth", align_bytes=64)
-        gmoved = keep.tile([P, S // 4], I32, name="gmoved", align_bytes=64)
-        nc.vector.memset(gmoved[:], 0)
-        for jh in range(2):
-            gs[0, jh] = gboth[:, W * jh : W * (jh + 1)]
-            gs[1, jh] = gmoved[:].bitcast(U8)[:, W * jh : W * (jh + 1)]
+        identity = keep.tile([P, P], F32, name="identity")
+        make_identity(nc, identity[:])
+        turned = sums.tile([P, P], F32, name="sum")
+        nc.tensor.transpose(turned[:], gain_square[:], identity[:])
+        gain_rows = keep.tile([P, P], F32, name="gain_rows")
+        nc.scalar.copy(gain_rows[:], turned[:])
+        gain_psum = gain_bank.tile([P, P], F32, name="gain_psum")
+        nc.tensor.transpose(gain_psum[:], gain_rows[:], identity[:])
+        gains_psum = gain_psum[:, 0:GAINS].rearrange("p (b t) -> p b t", t=PACK)
 
-        def gather_both(jh):
-            nc.vector.tensor_copy(gs[0, jh], tabs[:].bitcast(U8).indirect(offsets[:, 32 * jh : 32 * (jh + 1)]))
+        w1_raw, w1_bf16, w1_words, w1_plane, v_words = {}, {}, {}, {}, {}
 
-        def move_scales():
-            for q in range(4):
-                nc.sync.dma_start(
-                    out=gmoved[32 * q : 32 * q + 4, :], in_=gboth[:].bitcast(I32)[16 + 4 * q : 20 + 4 * q, :]
-                )
-
-        def pool_of(tag):
-            return ring if tag == "raw" else keep
-
-        ident = keep.tile([P, P], F32, name="ident")
-        make_identity(nc, ident[:])
-        g_t = ps.tile([P, P], F32, name="acc")
-        nc.tensor.transpose(g_t[:], gpad[:], ident[:])
-        g_rows = keep.tile([P, P], F32, name="g_rows")
-        nc.scalar.copy(g_rows[:], g_t[:])
-        g_ps = psg.tile([P, P], F32, name="g_ps")
-        nc.tensor.transpose(g_ps[:], g_rows[:], ident[:])
-        gains_v = g_ps[:, 0:8].rearrange("p (b t) -> p b t", t=4)
-
-        def load_w2_scales():
-            w2s = ring3.tile([P, 2, N // 4], I32, name="wg", align_bytes=64)
-            late["w2s"] = w2s
-            nc.vector.memset(w2s[:], 0)
-            for q in range(4):
-                nc.sync.dma_start(
-                    out=w2s[32 * q : 32 * q + 4, :, :],
-                    in_=w2_scales[:, 4 * q : 4 * q + 4, :].rearrange("a r c -> r a c").bitcast(I32),
-                )
-
-        def load_w2(tag):
-            late["w2w"] = pool_of(tag).tile([P, 2, N], I32, name=tag, align_bytes=64)
-            nc.sync.dma_start(out=late["w2w"][:], in_=w2_words.rearrange("a p c i -> p a (c i)").bitcast(I32))
-
-        def load_q(jh, tag):
-            qs[jh] = pool_of(tag).tile([P, 2, S], F32, name=tag, align_bytes=64)
+        def load_w1(a, b, tag):
+            w1_raw[a, b] = buffer(tag, [P, PACK, W], F32)
             nc.sync.dma_start(
-                out=qs[jh][:], in_=qg[2 * P * jh : 2 * P * (jh + 1), :].rearrange("(nt p) j -> p nt j", p=P)
+                out=w1_raw[a, b][:],
+                in_=w1[W * a : W * (a + 1), W * b : W * (b + 1)].rearrange("(p i) r -> p i r", i=PACK),
             )
 
         def gather_words(a, jh):
-            gw[a, jh] = keep.tile([P, W], U32, name="gw%d%d" % (a, jh), align_bytes=64)
-            nc.vector.tensor_copy(
-                gw[a, jh][:], tabw[a][:].bitcast(U32).indirect(offsets[:, 32 * jh : 32 * (jh + 1)])
-            )
+            v_words[a, jh] = keep.tile([P, W], U32, name="v_words%d%d" % (a, jh), align_bytes=64)
+            nc.vector.tensor_copy(v_words[a, jh][:], table[a][:].bitcast(U32).indirect(half_of_list(jh)))
 
-        def cast_w1(a, b, copy, lo=0, hi=P):
-            if (a, b) not in wg:
-                wg[a, b] = ring3.tile([P, 4 * W], BF16, name="wg", align_bytes=64)
-            copy(
-                wg[a, b][:].rearrange("p (t m i) -> p m i t", t=4, i=4)[:, lo:hi],
-                raw[a, b][:].rearrange("p i (m t) -> p m i t", t=4)[:, lo:hi],
-            )
+        def gather_scales():
+            for jh in range(2):
+                nc.vector.tensor_copy(
+                    picked_scales[:, W * jh : W * (jh + 1)], scale_window[:].bitcast(U8).indirect(half_of_list(jh))
+                )
+            for q in range(4):
+                nc.sync.dma_start(
+                    out=moved_scales[QUADRANT * q : QUADRANT * q + RUN, :],
+                    in_=picked_scales[:].bitcast(I32)[PASS1_ROW + RUN * q : PASS1_ROW + RUN * (q + 1), :],
+                )
 
-        def quant_w1(a, b):
-            w1c[a, b] = keep.tile([P, W], U32, name="w1c%d%d" % (a, b), align_bytes=64)
-            w1s[a, b] = keep.tile([P, W], U8, name="w1s%d%d" % (a, b), align_bytes=64)
-            nc.vector.quantize_mx(out=w1c[a, b][:].bitcast(E4), scales=w1s[a, b][:], in_=wg[a, b][:])
+        def round_w1(a, b):
+            w1_bf16[a, b] = rounded.tile([P, PACK * W], BF16, name="rounded", align_bytes=64)
+            dst = w1_bf16[a, b][:].rearrange("p (t m i) -> p m i t", t=PACK, i=PACK)
+            src = w1_raw[a, b][:].rearrange("p i (m t) -> p m i t", t=PACK)
+            cut = ROUND_ON_SCALAR[a, b]
+            if cut > 0:
+                nc.scalar.copy(dst[:, 0:cut], src[:, 0:cut])
+            if cut < P:
+                nc.vector.tensor_copy(dst[:, cut:P], src[:, cut:P])
 
-        def pass1(a, b, jh, t):
+        def quantise_w1(a, b):
+            w1_words[a, b] = keep.tile([P, W], U32, name="w1_words%d%d" % (a, b), align_bytes=64)
+            w1_plane[a, b] = keep.tile([P, W], U8, name="w1_plane%d%d" % (a, b), align_bytes=64)
+            nc.vector.quantize_mx(out=w1_words[a, b][:].bitcast(E4M3), scales=w1_plane[a, b][:], in_=w1_bf16[a, b][:])
+
+        a_sum, sigmoids, h_slots, h_bf16, h_words, h_plane = {}, {}, {}, {}, {}, {}
+
+        def first_product_pass(a, b, jh, t):
             if a == 0:
-                acc1[b, jh, t] = ps.tile([P, W], F32, name="acc")
+                a_sum[b, jh, t] = sums.tile([P, W], F32, name="sum")
             cols = slice(P * t, P * (t + 1))
             nc.tensor.matmul_mx(
-                out=acc1[b, jh, t][:],
-                lhsT=w1c[a, b][:, cols].bitcast(E4),
-                lhsT_scale=w1s[a, b][:, cols],
-                rhs=gw[a, jh][:].bitcast(E5),
-                rhs_scale=gs[a, jh],
+                out=a_sum[b, jh, t][:],
+                lhsT=w1_words[a, b][:, cols].bitcast(E4M3),
+                lhsT_scale=w1_plane[a, b][:, cols],
+                rhs=v_words[a, jh][:].bitcast(E5M2),
+                rhs_scale=v_plane[a][:, W * jh : W * (jh + 1)],
                 start=(a == 0),
                 stop=(a == 1),
             )
 
-        def sigmoid(b, jh, t, lo, hi):
-            if (b, jh) not in sig:
-                sig[b, jh] = ring4.tile([P, 4, W], F32, name="sig")
+        def sigmoid(b, jh, t):
+            if t == 0:
+                sigmoids[b, jh] = hidden.tile([P, PACK, W], F32, name="sigmoids")
             nc.scalar.activation(
-                sig[b, jh][:, t, lo:hi], acc1[b, jh, t][:, lo:hi], ACT.Sigmoid, bias=bias[:, b, t : t + 1]
+                sigmoids[b, jh][:, t, :], a_sum[b, jh, t][:], ACT.Sigmoid, bias=bias[:, b, t : t + 1]
             )
 
-        def open1(b, jh, ts):
-            for t in ts:
-                pass1(0, b, jh, t)
+        def finish_group(b, jh):
+            for t in SLOTS:
+                if (b, jh, t) not in a_sum:
+                    first_product_pass(0, b, jh, t)
+                first_product_pass(1, b, jh, t)
+                sigmoid(b, jh, t)
 
-        def close1(b, jh):
-            for t in range(4):
-                if (b, jh, t) not in acc1:
-                    pass1(0, b, jh, t)
-                pass1(1, b, jh, t)
-                sigmoid(b, jh, t, 0, W)
+        def h_columns(b, jh, lo, hi):
+            if (b, jh) not in h_bf16:
+                h_bf16[b, jh] = hidden.tile([P, PACK * W], BF16, name="h_bf16", align_bytes=64)
+            return h_bf16[b, jh][:, PACK * lo : PACK * hi]
 
-        def apply_gain(b, jh, lo, hi, engine, g):
-            if (b, jh) not in hb:
-                hb[b, jh] = ring4.tile([P, 4 * W], BF16, name="hb", align_bytes=64)
-            engine.tensor_tensor(
-                hb[b, jh][:, 4 * lo : 4 * hi].rearrange("p (c i t) -> p c t i", i=4, t=4),
-                sig[b, jh][:, :, lo:hi].rearrange("p t (c i) -> p c t i", i=4),
-                g[:, b, :].unsqueeze(1).unsqueeze(3).to_broadcast([P, (hi - lo) // 4, 4, 4]),
-                MULT,
-            )
-
-        def gain_v(b, jh, lo, hi):
-            apply_gain(b, jh, lo, hi, nc.vector, gains_v)
-
-        def gain_g(b, jh, lo, hi):
-            if (b, jh) not in hb:
-                hb[b, jh] = ring4.tile([P, 4 * W], BF16, name="hb", align_bytes=64)
-            nc.gpsimd.tensor_tensor(
-                hb[b, jh][:, 4 * lo : 4 * hi].rearrange("p (n t) -> p n t", t=4),
-                sig[b, jh][:, :, lo:hi].rearrange("p t n -> p n t"),
-                gains[:, b, :].unsqueeze(1).to_broadcast([P, hi - lo, 4]),
-                MULT,
-            )
-
-        def gain_s(b, jh, lo, hi):
-            if (b, jh) not in prod:
-                prod[b, jh] = keep.tile([P, 4, W], BF16, name="hp%d%d" % (b, jh), align_bytes=64)
-            for t in range(4):
-                nc.scalar.activation(
-                    prod[b, jh][:, t, lo:hi], sig[b, jh][:, t, lo:hi], ACT.Copy, scale=gains[:, b, t : t + 1]
+        def gain_beside_vector(b, jh):
+            v, g = GAIN_CUTS[b, jh]
+            for lo in range(v, g, GPSIMD_COLS):
+                hi = min(g, lo + GPSIMD_COLS)
+                nc.gpsimd.tensor_tensor(
+                    h_columns(b, jh, lo, hi).rearrange("p (n t) -> p n t", t=PACK),
+                    sigmoids[b, jh][:, :, lo:hi].rearrange("p t n -> p n t"),
+                    gains[:, b, :].unsqueeze(1).to_broadcast([P, hi - lo, PACK]),
+                    MULT,
                 )
-
-        def inter_v(b, jh, lo, hi):
-            if (b, jh) not in hb:
-                hb[b, jh] = ring4.tile([P, 4 * W], BF16, name="hb", align_bytes=64)
-            nc.vector.tensor_copy(
-                hb[b, jh][:, 4 * lo : 4 * hi].rearrange("p (c i t) -> p c t i", i=4, t=4),
-                prod[b, jh][:, :, lo:hi].rearrange("p t (c i) -> p c t i", i=4),
-            )
-
-        def quant_h(b, jh, lo, hi):
-            if (b, jh) not in hc:
-                hc[b, jh] = keep.tile([P, W], U32, name="hc%d%d" % (b, jh), align_bytes=64)
-                hs[b, jh] = keep.tile([P, W], U8, name="hs%d%d" % (b, jh), align_bytes=64)
-            nc.vector.quantize_mx(
-                out=hc[b, jh][:, lo:hi].bitcast(E4), scales=hs[b, jh][:, lo:hi], in_=hb[b, jh][:, 4 * lo : 4 * hi]
-            )
-
-        def product2(jh, lo, hi, nts):
-            bank = ps.tile([P, len(nts), hi - lo], F32, name="acc")
-            acc2[jh, lo, nts[0]] = bank
-            for u, nt in enumerate(nts):
-                for b in range(2):
-                    nc.tensor.matmul_mx(
-                        out=bank[:, u, :],
-                        lhsT=late["w2w"][:, b, P * nt : P * (nt + 1)].bitcast(E4),
-                        lhsT_scale=late["w2s"][:, b, :].bitcast(U8)[:, P * nt : P * (nt + 1)],
-                        rhs=hc[b, jh][:, lo:hi].bitcast(E4),
-                        rhs_scale=hs[b, jh][:, lo:hi],
-                        start=(b == 0),
-                        stop=(b == 1),
+            if g < W:
+                h_slots[b, jh] = keep.tile([P, PACK, W], BF16, name="h_slots%d%d" % (b, jh), align_bytes=64)
+                for t in SLOTS:
+                    nc.scalar.activation(
+                        h_slots[b, jh][:, t, g:W], sigmoids[b, jh][:, t, g:W], ACT.Copy, scale=gains[:, b, t : t + 1]
                     )
 
-        def evac(jh, nt):
-            y = keep.tile([P, W], F32, name="y%d%d" % (jh, nt))
-            nc.scalar.copy(y[:], acc2[jh, 0, nt][:, 0, :])
-            prod["g", nt] = keep.tile([P, W], F32, name="gprod%d%d" % (jh, nt))
-            nc.gpsimd.tensor_tensor(prod["g", nt][:], y[:], qs[nt // 2][:, nt % 2, W * jh : W * (jh + 1)], MULT)
-
-        def absout(jh, nt):
-            res = keep.tile([P, W], F32, name="gres%d%d" % (jh, nt))
-            nc.scalar.activation(res[:], prod["g", nt][:], ACT.Abs)
-            nc.sync.dma_start(out=out[P * nt : P * (nt + 1), W * jh : W * (jh + 1)], in_=res[:])
-
-        def finish(jh, lo, hi, nts):
-            shape = [P, len(nts), hi - lo]
-            tag = "%d_%d_%d" % (jh, lo, nts[0])
-            product = keep.tile(shape, F32, name="prod" + tag)
+        def gain_on_vector(b, jh):
+            v, g = GAIN_CUTS[b, jh]
             nc.vector.tensor_tensor(
-                product[:], acc2[jh, lo, nts[0]][:], qs[nts[0] // 2][:, nts[0] % 2 : nts[-1] % 2 + 1, W * jh + lo : W * jh + hi], MULT
+                h_columns(b, jh, 0, v).rearrange("p (c i t) -> p c t i", i=LINE, t=PACK),
+                sigmoids[b, jh][:, :, 0:v].rearrange("p t (c i) -> p c t i", i=LINE),
+                gains_psum[:, b, :].unsqueeze(1).unsqueeze(3).to_broadcast([P, v // LINE, PACK, LINE]),
+                MULT,
             )
-            res = keep.tile(shape, F32, name="res" + tag)
-            nc.scalar.activation(res[:], product[:], ACT.Abs)
+            if g < W:
+                nc.vector.tensor_copy(
+                    h_columns(b, jh, g, W).rearrange("p (c i t) -> p c t i", i=LINE, t=PACK),
+                    h_slots[b, jh][:, :, g:W].rearrange("p t (c i) -> p c t i", i=LINE),
+                )
+
+        def quantise_h(b, jh):
+            h_words[b, jh] = keep.tile([P, W], U32, name="h_words%d%d" % (b, jh), align_bytes=64)
+            h_plane[b, jh] = keep.tile([P, W], U8, name="h_plane%d%d" % (b, jh), align_bytes=64)
+            nc.vector.quantize_mx(out=h_words[b, jh][:].bitcast(E4M3), scales=h_plane[b, jh][:], in_=h_bf16[b, jh][:])
+
+        w2, q_rows, y_sum = {}, {}, {}
+
+        def load_w2_words():
+            w2["words"] = buffer("words1", [P, 2, N], I32)
+            nc.sync.dma_start(out=w2["words"][:], in_=w2_words.rearrange("b p c i -> p b (c i)").bitcast(I32))
+
+        def load_w2_planes():
+            w2["planes"] = rounded.tile([P, 2, N // 4], I32, name="rounded", align_bytes=64)
+            nc.vector.memset(w2["planes"][:], 0)
+            for q in range(4):
+                nc.sync.dma_start(
+                    out=w2["planes"][QUADRANT * q : QUADRANT * q + RUN, :, :],
+                    in_=w2_scales[:, RUN * q : RUN * (q + 1), :].rearrange("b r c -> r b c").bitcast(I32),
+                )
+
+        def load_q(pair):
+            q_rows[pair] = buffer("stage", [P, 2, S], F32)
             nc.sync.dma_start(
-                out=out[P * nts[0] : P * (nts[-1] + 1), W * jh + lo : W * jh + hi].rearrange(
-                    "(u p) j -> p u j", p=P
-                ),
-                in_=res[:],
+                out=q_rows[pair][:], in_=qg[2 * P * pair : 2 * P * (pair + 1), :].rearrange("(u p) j -> p u j", p=P)
             )
 
-        load_w1(0, 0)
-        load_w1(1, 0)
-        load_tab(1)
-        gather_both(0)
-        gather_both(1)
-        move_scales()
-        load_w1(0, 1)
+        def second_product(jh, nt):
+            y_sum[jh, nt] = sums.tile([P, W], F32, name="sum")
+            cols = slice(P * nt, P * (nt + 1))
+            for b in range(2):
+                nc.tensor.matmul_mx(
+                    out=y_sum[jh, nt][:],
+                    lhsT=w2["words"][:, b, cols].bitcast(E4M3),
+                    lhsT_scale=w2["planes"][:, b, :].bitcast(U8)[:, cols],
+                    rhs=h_words[b, jh][:].bitcast(E4M3),
+                    rhs_scale=h_plane[b, jh][:],
+                    start=(b == 0),
+                    stop=(b == 1),
+                )
+
+        def times_q(jh, nt, engine, y):
+            product = keep.tile([P, W], F32, name="product%d%d" % (jh, nt))
+            engine.tensor_tensor(product[:], y[:], q_rows[nt // 2][:, nt % 2, W * jh : W * (jh + 1)], MULT)
+            return product
+
+        def store_abs(jh, nt, product):
+            result = keep.tile([P, W], F32, name="result%d%d" % (jh, nt))
+            nc.scalar.activation(result[:], product[:], ACT.Abs)
+            nc.sync.dma_start(out=out[P * nt : P * (nt + 1), W * jh : W * (jh + 1)], in_=result[:])
+
+        def finish_tile(jh, nt):
+            store_abs(jh, nt, times_q(jh, nt, nc.vector, y_sum[jh, nt]))
+
+        load_w1(0, 0, "stage")
+        load_w1(1, 0, "stage")
+        load_table(1, "words1")
+        gather_scales()
+        load_w1(0, 1, "scale_window")
         gather_words(0, 1)
         gather_words(0, 0)
-        cast_w1(0, 0, nc.scalar.copy, 0, 128)
-        load_w1(1, 1)
-        quant_w1(0, 0)
-        pass1(0, 0, 0, 0)
-        pass1(0, 0, 0, 1)
-        pass1(0, 0, 0, 2)
-        pass1(0, 0, 0, 3)
-        pass1(0, 0, 1, 0)
-        pass1(0, 0, 1, 1)
-        pass1(0, 0, 1, 2)
-        cast_w1(1, 0, nc.scalar.copy, 0, 48)
-        cast_w1(1, 0, nc.vector.tensor_copy, 48, 128)
-        load_q(0, "raw")
-        quant_w1(1, 0)
+        round_w1(0, 0)
+        load_w1(1, 1, "stage")
+        quantise_w1(0, 0)
+        for bank in range(SUM_BANKS):
+            first_product_pass(0, 0, bank // PACK, bank % PACK)
+        round_w1(1, 0)
+        load_q(0)
+        quantise_w1(1, 0)
         gather_words(1, 0)
-        pass1(1, 0, 0, 0)
-        pass1(1, 0, 0, 1)
-        pass1(1, 0, 0, 2)
-        pass1(1, 0, 0, 3)
+        for t in SLOTS:
+            first_product_pass(1, 0, 0, t)
         gather_words(1, 1)
-        cast_w1(0, 1, nc.scalar.copy, 0, 32)
-        cast_w1(0, 1, nc.vector.tensor_copy, 32, 128)
-        load_w2("tabw")
-        sigmoid(0, 0, 0, 0, 512)
-        sigmoid(0, 0, 1, 0, 512)
-        sigmoid(0, 0, 2, 0, 512)
-        sigmoid(0, 0, 3, 0, 512)
-        quant_w1(0, 1)
-        cast_w1(1, 1, nc.scalar.copy, 0, 32)
-        cast_w1(1, 1, nc.vector.tensor_copy, 32, 128)
-        load_q(1, "raw")
-        load_w2_scales()
-        quant_w1(1, 1)
-        pass1(1, 0, 1, 0)
-        sigmoid(0, 1, 0, 0, 512)
-        pass1(1, 0, 1, 1)
-        sigmoid(0, 1, 1, 0, 512)
-        pass1(1, 0, 1, 2)
-        sigmoid(0, 1, 2, 0, 512)
-        pass1(0, 0, 1, 3)
-        pass1(1, 0, 1, 3)
-        sigmoid(0, 1, 3, 0, 512)
-        gain_g(0, 0, 384, 512)
-        gain_g(0, 1, 256, 384)
-        gain_g(0, 1, 384, 512)
-        pass1(0, 1, 0, 0)
-        pass1(1, 1, 0, 0)
-        sigmoid(1, 0, 0, 0, 512)
-        pass1(0, 1, 0, 1)
-        pass1(1, 1, 0, 1)
-        sigmoid(1, 0, 1, 0, 512)
-        pass1(0, 1, 0, 2)
-        pass1(1, 1, 0, 2)
-        sigmoid(1, 0, 2, 0, 512)
-        pass1(0, 1, 0, 3)
-        pass1(1, 1, 0, 3)
-        sigmoid(1, 0, 3, 0, 512)
-        gain_g(1, 0, 256, 384)
-        gain_s(1, 0, 384, 512)
-        pass1(0, 1, 1, 0)
-        pass1(1, 1, 1, 0)
-        sigmoid(1, 1, 0, 0, 512)
-        pass1(0, 1, 1, 1)
-        pass1(1, 1, 1, 1)
-        sigmoid(1, 1, 1, 0, 512)
-        pass1(0, 1, 1, 2)
-        pass1(1, 1, 1, 2)
-        sigmoid(1, 1, 2, 0, 512)
-        pass1(0, 1, 1, 3)
-        pass1(1, 1, 1, 3)
-        sigmoid(1, 1, 3, 0, 512)
-        gain_g(1, 1, 384, 512)
-        gain_v(0, 0, 0, 384)
-        gain_v(0, 1, 0, 256)
-        quant_h(0, 0, 0, 512)
-        gain_v(1, 0, 0, 256)
-        inter_v(1, 0, 384, 512)
-        quant_h(1, 0, 0, 512)
-        quant_h(0, 1, 0, 512)
-        product2(0, 0, 512, [0])
-        product2(0, 0, 512, [1])
-        product2(0, 0, 512, [2])
-        product2(0, 0, 512, [3])
-        evac(0, 0)
-        gain_v(1, 1, 0, 384)
-        absout(0, 0)
-        finish(0, 0, 512, [1])
-        quant_h(1, 1, 0, 512)
-        finish(0, 0, 512, [2])
-        finish(0, 0, 512, [3])
-        product2(1, 0, 512, [0])
-        finish(1, 0, 512, [0])
-        product2(1, 0, 512, [1])
-        finish(1, 0, 512, [1])
-        product2(1, 0, 512, [2])
-        finish(1, 0, 512, [2])
-        product2(1, 0, 512, [3])
-        finish(1, 0, 512, [3])
+
+        round_w1(0, 1)
+        load_w2_words()
+        for t in SLOTS:
+            sigmoid(0, 0, t)
+        quantise_w1(0, 1)
+        round_w1(1, 1)
+        load_q(1)
+        load_w2_planes()
+        quantise_w1(1, 1)
+        finish_group(0, 1)
+        gain_beside_vector(0, 0)
+        gain_beside_vector(0, 1)
+        for jh in range(2):
+            finish_group(1, jh)
+            gain_beside_vector(1, jh)
+
+        gain_on_vector(0, 0)
+        gain_on_vector(0, 1)
+        quantise_h(0, 0)
+        gain_on_vector(1, 0)
+        quantise_h(1, 0)
+        quantise_h(0, 1)
+        for nt in ROW_TILES:
+            second_product(0, nt)
+        y_copy = keep.tile([P, W], F32, name="y_copy")
+        nc.scalar.copy(y_copy[:], y_sum[0, 0][:])
+        gpsimd_product = times_q(0, 0, nc.gpsimd, y_copy)
+        gain_on_vector(1, 1)
+        store_abs(0, 0, gpsimd_product)
+        finish_tile(0, 1)
+        quantise_h(1, 1)
+        finish_tile(0, 2)
+        finish_tile(0, 3)
+        for nt in ROW_TILES:
+            second_product(1, nt)
+            finish_tile(1, nt)

from contextlib import ExitStack

import concourse.mybir as mybir
from concourse.masks import make_identity

K, T, S, H, N = 1024, 2048, 1024, 1024, 512
FLOPS = 2 * K * H * S + 2 * H * N * S

F32 = mybir.dt.float32
BF16 = mybir.dt.bfloat16
I32 = mybir.dt.int32
U32 = mybir.dt.uint32
U16 = mybir.dt.uint16
U8 = mybir.dt.uint8
E4M3 = mybir.dt.float8_e4m3fn_x4
E5M2 = mybir.dt.float8_e5m2_x4
ACT = mybir.ActivationFunctionType
MULT = mybir.AluOpType.mult

P = 128
PACK = 4
W = 512
LIST_COLS = W // 16
QUADRANT = 32
RUN = 4
PASS1_ROW = 16
LINE = 4
SLOTS = range(PACK)
ROW_TILES = range(N // P)
GAINS = 2 * PACK
SUM_BANKS = 7

ROUND_ON_SCALAR = {(0, 0): 128, (1, 0): 48, (0, 1): 32, (1, 1): 32}
GAIN_CUTS = {(0, 0): (384, 512), (0, 1): (256, 512), (1, 0): (256, 384), (1, 1): (384, 512)}
GPSIMD_COLS = 128


def tile_list_coordinate_influence_retrieval_kernel(
    tc, tab_words, tab_scales, offs, w1, b1, gain, w2_words, w2_scales, qg, out
):
    nc = tc.nc
    with ExitStack() as ctx:
        keep = ctx.enter_context(tc.tile_pool(name="keep", bufs=1))
        stage = ctx.enter_context(tc.tile_pool(name="stage", bufs=2))
        rounded = ctx.enter_context(tc.tile_pool(name="rounded", bufs=3))
        hidden = ctx.enter_context(tc.tile_pool(name="hidden", bufs=4))
        sums = ctx.enter_context(tc.psum_pool(name="sums", bufs=SUM_BANKS))
        gain_bank = ctx.enter_context(tc.psum_pool(name="gain_bank", bufs=1))

        def buffer(tag, shape, dtype):
            return (stage if tag == "stage" else keep).tile(shape, dtype, name=tag, align_bytes=64)

        offsets = keep.tile([P, S // 16], U16, name="offsets")
        nc.sync.dma_start(offsets[:], offs)

        def half_of_list(jh):
            return offsets[:, LIST_COLS * jh : LIST_COLS * (jh + 1)]

        table = {}

        def load_table(a, tag):
            table[a] = buffer(tag, [P, T], I32)
            nc.sync.dma_start(out=table[a][:], in_=tab_words[a].rearrange("p t i -> p (t i)").bitcast(I32))

        filler_in = buffer("words1", [P, P - GAINS], F32)
        filler_bias = buffer("stage", [P, 1], F32)
        filler_scale = buffer("stage", [P, 1], F32)

        scale_window = buffer("scale_window", [P, T // 4], I32)
        nc.vector.memset(scale_window[:], 0)
        load_table(0, "words0")
        bias = keep.tile([P, 2, PACK], F32, name="bias")
        nc.scalar.dma_start(out=bias[:], in_=b1.rearrange("(b p t) -> p b t", p=P, t=PACK))
        gain_square = keep.tile([P, P], F32, name="gain_square")
        gains = gain_square[:, 0:GAINS].rearrange("p (b t) -> p b t", t=PACK)
        nc.scalar.dma_start(out=gains, in_=gain.rearrange("(b p t) -> p b t", p=P, t=PACK))
        scale_rows = tab_scales.rearrange("a q t -> (a q) t").bitcast(I32)
        nc.sync.dma_start(out=scale_window[0:QUADRANT, :], in_=scale_rows)
        for q in range(1, 4):
            nc.sync.dma_start(
                out=scale_window[QUADRANT * q : QUADRANT * q + RUN, :], in_=scale_rows[RUN * q : RUN * (q + 1), :]
            )

        nc.vector.memset(filler_in[:], 0.0)
        nc.vector.memset(filler_bias[:], 0.0)
        nc.vector.memset(filler_scale[:], 1.0)
        nc.scalar.activation(
            gain_square[:, GAINS:], filler_in[:], ACT.Sigmoid, bias=filler_bias[:], scale=filler_scale[:]
        )

        picked_scales = keep.tile([P, S], U8, name="picked_scales", align_bytes=64)
        moved_scales = keep.tile([P, S // 4], I32, name="moved_scales", align_bytes=64)
        nc.vector.memset(moved_scales[:], 0)
        v_plane = {0: picked_scales[:], 1: moved_scales[:].bitcast(U8)}

        identity = keep.tile([P, P], F32, name="identity")
        make_identity(nc, identity[:])
        turned = sums.tile([P, P], F32, name="sum")
        nc.tensor.transpose(turned[:], gain_square[:], identity[:])
        gain_rows = keep.tile([P, P], F32, name="gain_rows")
        nc.scalar.copy(gain_rows[:], turned[:])
        gain_psum = gain_bank.tile([P, P], F32, name="gain_psum")
        nc.tensor.transpose(gain_psum[:], gain_rows[:], identity[:])
        gains_psum = gain_psum[:, 0:GAINS].rearrange("p (b t) -> p b t", t=PACK)

        w1_raw, w1_bf16, w1_words, w1_plane, v_words = {}, {}, {}, {}, {}

        def load_w1(a, b, tag):
            w1_raw[a, b] = buffer(tag, [P, PACK, W], F32)
            nc.sync.dma_start(
                out=w1_raw[a, b][:],
                in_=w1[W * a : W * (a + 1), W * b : W * (b + 1)].rearrange("(p i) r -> p i r", i=PACK),
            )

        def gather_words(a, jh):
            v_words[a, jh] = keep.tile([P, W], U32, name="v_words%d%d" % (a, jh), align_bytes=64)
            nc.vector.tensor_copy(v_words[a, jh][:], table[a][:].bitcast(U32).indirect(half_of_list(jh)))

        def gather_scales():
            for jh in range(2):
                nc.vector.tensor_copy(
                    picked_scales[:, W * jh : W * (jh + 1)], scale_window[:].bitcast(U8).indirect(half_of_list(jh))
                )
            for q in range(4):
                nc.sync.dma_start(
                    out=moved_scales[QUADRANT * q : QUADRANT * q + RUN, :],
                    in_=picked_scales[:].bitcast(I32)[PASS1_ROW + RUN * q : PASS1_ROW + RUN * (q + 1), :],
                )

        def round_w1(a, b):
            w1_bf16[a, b] = rounded.tile([P, PACK * W], BF16, name="rounded", align_bytes=64)
            dst = w1_bf16[a, b][:].rearrange("p (t m i) -> p m i t", t=PACK, i=PACK)
            src = w1_raw[a, b][:].rearrange("p i (m t) -> p m i t", t=PACK)
            cut = ROUND_ON_SCALAR[a, b]
            if cut > 0:
                nc.scalar.copy(dst[:, 0:cut], src[:, 0:cut])
            if cut < P:
                nc.vector.tensor_copy(dst[:, cut:P], src[:, cut:P])

        def quantise_w1(a, b):
            w1_words[a, b] = keep.tile([P, W], U32, name="w1_words%d%d" % (a, b), align_bytes=64)
            w1_plane[a, b] = keep.tile([P, W], U8, name="w1_plane%d%d" % (a, b), align_bytes=64)
            nc.vector.quantize_mx(out=w1_words[a, b][:].bitcast(E4M3), scales=w1_plane[a, b][:], in_=w1_bf16[a, b][:])

        a_sum, sigmoids, h_slots, h_bf16, h_words, h_plane = {}, {}, {}, {}, {}, {}

        def first_product_pass(a, b, jh, t):
            if a == 0:
                a_sum[b, jh, t] = sums.tile([P, W], F32, name="sum")
            cols = slice(P * t, P * (t + 1))
            nc.tensor.matmul_mx(
                out=a_sum[b, jh, t][:],
                lhsT=w1_words[a, b][:, cols].bitcast(E4M3),
                lhsT_scale=w1_plane[a, b][:, cols],
                rhs=v_words[a, jh][:].bitcast(E5M2),
                rhs_scale=v_plane[a][:, W * jh : W * (jh + 1)],
                start=(a == 0),
                stop=(a == 1),
            )

        def sigmoid(b, jh, t):
            if t == 0:
                sigmoids[b, jh] = hidden.tile([P, PACK, W], F32, name="sigmoids")
            nc.scalar.activation(
                sigmoids[b, jh][:, t, :], a_sum[b, jh, t][:], ACT.Sigmoid, bias=bias[:, b, t : t + 1]
            )

        def finish_group(b, jh):
            for t in SLOTS:
                if (b, jh, t) not in a_sum:
                    first_product_pass(0, b, jh, t)
                first_product_pass(1, b, jh, t)
                sigmoid(b, jh, t)

        def h_columns(b, jh, lo, hi):
            if (b, jh) not in h_bf16:
                h_bf16[b, jh] = hidden.tile([P, PACK * W], BF16, name="h_bf16", align_bytes=64)
            return h_bf16[b, jh][:, PACK * lo : PACK * hi]

        def gain_beside_vector(b, jh):
            v, g = GAIN_CUTS[b, jh]
            for lo in range(v, g, GPSIMD_COLS):
                hi = min(g, lo + GPSIMD_COLS)
                nc.gpsimd.tensor_tensor(
                    h_columns(b, jh, lo, hi).rearrange("p (n t) -> p n t", t=PACK),
                    sigmoids[b, jh][:, :, lo:hi].rearrange("p t n -> p n t"),
                    gains[:, b, :].unsqueeze(1).to_broadcast([P, hi - lo, PACK]),
                    MULT,
                )
            if g < W:
                h_slots[b, jh] = keep.tile([P, PACK, W], BF16, name="h_slots%d%d" % (b, jh), align_bytes=64)
                for t in SLOTS:
                    nc.scalar.activation(
                        h_slots[b, jh][:, t, g:W], sigmoids[b, jh][:, t, g:W], ACT.Copy, scale=gains[:, b, t : t + 1]
                    )

        def gain_on_vector(b, jh):
            v, g = GAIN_CUTS[b, jh]
            nc.vector.tensor_tensor(
                h_columns(b, jh, 0, v).rearrange("p (c i t) -> p c t i", i=LINE, t=PACK),
                sigmoids[b, jh][:, :, 0:v].rearrange("p t (c i) -> p c t i", i=LINE),
                gains_psum[:, b, :].unsqueeze(1).unsqueeze(3).to_broadcast([P, v // LINE, PACK, LINE]),
                MULT,
            )
            if g < W:
                nc.vector.tensor_copy(
                    h_columns(b, jh, g, W).rearrange("p (c i t) -> p c t i", i=LINE, t=PACK),
                    h_slots[b, jh][:, :, g:W].rearrange("p t (c i) -> p c t i", i=LINE),
                )

        def quantise_h(b, jh):
            h_words[b, jh] = keep.tile([P, W], U32, name="h_words%d%d" % (b, jh), align_bytes=64)
            h_plane[b, jh] = keep.tile([P, W], U8, name="h_plane%d%d" % (b, jh), align_bytes=64)
            nc.vector.quantize_mx(out=h_words[b, jh][:].bitcast(E4M3), scales=h_plane[b, jh][:], in_=h_bf16[b, jh][:])

        w2, q_rows, y_sum = {}, {}, {}

        def load_w2_words():
            w2["words"] = buffer("words1", [P, 2, N], I32)
            nc.sync.dma_start(out=w2["words"][:], in_=w2_words.rearrange("b p c i -> p b (c i)").bitcast(I32))

        def load_w2_planes():
            w2["planes"] = rounded.tile([P, 2, N // 4], I32, name="rounded", align_bytes=64)
            nc.vector.memset(w2["planes"][:], 0)
            for q in range(4):
                nc.sync.dma_start(
                    out=w2["planes"][QUADRANT * q : QUADRANT * q + RUN, :, :],
                    in_=w2_scales[:, RUN * q : RUN * (q + 1), :].rearrange("b r c -> r b c").bitcast(I32),
                )

        def load_q(pair):
            q_rows[pair] = buffer("stage", [P, 2, S], F32)
            nc.sync.dma_start(
                out=q_rows[pair][:], in_=qg[2 * P * pair : 2 * P * (pair + 1), :].rearrange("(u p) j -> p u j", p=P)
            )

        def second_product(jh, nt):
            y_sum[jh, nt] = sums.tile([P, W], F32, name="sum")
            cols = slice(P * nt, P * (nt + 1))
            for b in range(2):
                nc.tensor.matmul_mx(
                    out=y_sum[jh, nt][:],
                    lhsT=w2["words"][:, b, cols].bitcast(E4M3),
                    lhsT_scale=w2["planes"][:, b, :].bitcast(U8)[:, cols],
                    rhs=h_words[b, jh][:].bitcast(E4M3),
                    rhs_scale=h_plane[b, jh][:],
                    start=(b == 0),
                    stop=(b == 1),
                )

        def times_q(jh, nt, engine, y):
            product = keep.tile([P, W], F32, name="product%d%d" % (jh, nt))
            engine.tensor_tensor(product[:], y[:], q_rows[nt // 2][:, nt % 2, W * jh : W * (jh + 1)], MULT)
            return product

        def store_abs(jh, nt, product):
            result = keep.tile([P, W], F32, name="result%d%d" % (jh, nt))
            nc.scalar.activation(result[:], product[:], ACT.Abs)
            nc.sync.dma_start(out=out[P * nt : P * (nt + 1), W * jh : W * (jh + 1)], in_=result[:])

        def finish_tile(jh, nt):
            store_abs(jh, nt, times_q(jh, nt, nc.vector, y_sum[jh, nt]))

        load_w1(0, 0, "stage")
        load_w1(1, 0, "stage")
        load_table(1, "words1")
        gather_scales()
        load_w1(0, 1, "scale_window")
        gather_words(0, 1)
        gather_words(0, 0)
        round_w1(0, 0)
        load_w1(1, 1, "stage")
        quantise_w1(0, 0)
        for bank in range(SUM_BANKS):
            first_product_pass(0, 0, bank // PACK, bank % PACK)
        round_w1(1, 0)
        load_q(0)
        quantise_w1(1, 0)
        gather_words(1, 0)
        for t in SLOTS:
            first_product_pass(1, 0, 0, t)
        gather_words(1, 1)

        round_w1(0, 1)
        load_w2_words()
        for t in SLOTS:
            sigmoid(0, 0, t)
        quantise_w1(0, 1)
        round_w1(1, 1)
        load_q(1)
        load_w2_planes()
        quantise_w1(1, 1)
        finish_group(0, 1)
        gain_beside_vector(0, 0)
        gain_beside_vector(0, 1)
        for jh in range(2):
            finish_group(1, jh)
            gain_beside_vector(1, jh)

        gain_on_vector(0, 0)
        gain_on_vector(0, 1)
        quantise_h(0, 0)
        gain_on_vector(1, 0)
        quantise_h(1, 0)
        quantise_h(0, 1)
        for nt in ROW_TILES:
            second_product(0, nt)
        y_copy = keep.tile([P, W], F32, name="y_copy")
        nc.scalar.copy(y_copy[:], y_sum[0, 0][:])
        gpsimd_product = times_q(0, 0, nc.gpsimd, y_copy)
        gain_on_vector(1, 1)
        store_abs(0, 0, gpsimd_product)
        finish_tile(0, 1)
        quantise_h(1, 1)
        finish_tile(0, 2)
        finish_tile(0, 3)
        for nt in ROW_TILES:
            second_product(1, nt)
            finish_tile(1, nt)
